import numpy as np, ml_dtypes
CORES = [1,5,17,21,33,37,49,53]
N = 8
BF = ml_dtypes.bfloat16
L, S, Q = 256, 4, 1024
def packed(rng, st):
    fr = np.diff(np.append(st, 2048)); sy = rng.permutation(256)[:len(st)]
    return np.stack([np.repeat(2048 * (fr - 1) + st, fr), np.repeat(sy, fr)])
def model(rng, n):
    return packed(rng, np.concatenate([[0], np.sort(rng.integers(0, 2048 - 8 * n + 1, n - 1)) + 8 * np.arange(1, n)]).astype(np.int64))
def both(m):
    return {"models": np.ascontiguousarray(m[:, :, 0]).astype(np.int32), "letters": np.ascontiguousarray(m[:, :, 1]).astype(np.int32)}
def models_of(rng, n):
    return both(np.stack([np.stack([model(rng, int(n[r, g])) for g in range(8)]) for r in range(N)]))
def some_states(rng):
    return np.clip(np.exp2(12 + 8 * rng.random((N, 8, L))), 4096, 1048575).astype(np.int32)
def some_bytes(rng):
    return rng.integers(0, 256, (N, 8, Q)).astype(np.int32)
def same(p):
    return np.repeat(p[None], N, axis=0).astype(np.int32)
def some_places(rng):
    return same(np.stack([rng.permutation(N * Q) for g in range(8)]))
def setup_inputs(rng):
    n = np.exp2(1 + 6.5 * rng.random((N, 8))).astype(np.int64); n[:, rng.integers(0, 8)] = 256
    m = models_of(rng, n)
    return {"states": some_states(rng), "models": m["models"], "letters": m["letters"], "stock": some_bytes(rng), "places": some_places(rng)}
def setup_inputs_every(rng):
    x = some_states(rng); x[:, :, 0] = 4096; x[:, :, L - 1] = 1048575
    m = models_of(rng, np.full((N, 8), 256)); p = some_places(rng); g = rng.permutation(8)
    p[:, g[0]] = np.arange(N * Q); p[:, g[1]] = np.arange(N * Q)[::-1]
    return {"states": x, "models": m["models"], "letters": m["letters"], "stock": some_bytes(rng), "places": p}
def setup_inputs_dry(rng):
    d = setup_inputs(rng); n = np.exp2(1 + 6.5 * rng.random((N, 8))).astype(np.int64); g = rng.permutation(8); p = rng.permutation(N)
    n[:, g[:3]] = 1
    for i in range(5):
        n[p[i % N], g[3 + i]] = 1
    d.update(models_of(rng, n)); return d
def setup_inputs_edge(rng):
    k = 2 ** rng.integers(4, 11, (N, 8, 1)); up = 4096 // k; a = rng.integers(0, 2048, (N, 8, L)) // k * k
    kind = rng.integers(0, 4, (N, 8, L)); kind[:, :, :4] = np.arange(4)
    x = np.where(kind == 0, 2048 * up + a, np.where(kind == 1, 2048 * (up - 1) + a + k - 1, np.where(kind == 2, 4096, 1048575)))
    m = both(np.stack([np.stack([packed(rng, np.arange(0, 2048, int(k[r, g, 0]))) for g in range(8)]) for r in range(N)]))
    return {"states": x.astype(np.int32), "models": m["models"], "letters": m["letters"], "stock": (255 * rng.integers(0, 2, (N, 8, Q))).astype(np.int32), "places": some_places(rng)}
def setup_inputs_few(rng):
    x = rng.integers(2 ** 19, 2 ** 20, (N, 8, L)); x[:, :, 0] = rng.integers(4096, 8192, (N, 8)); x[:, :, L - 1] = rng.integers(4096, 8192, (N, 8)); x[:, :, 1] = rng.integers(8192, 16384, (N, 8))
    p = rng.permutation(N); m = both(np.stack([np.stack([packed(rng, np.arange(0, 2048, 8 if p[g % N] == r else 1024)) for g in range(8)]) for r in range(N)]))
    return {"states": x.astype(np.int32), "models": m["models"], "letters": m["letters"], "stock": some_bytes(rng), "places": some_places(rng)}
def setup_inputs_spread(rng):
    slot = np.arange(2048); e = np.floor((slot + 1) * rng.random((N, 8, 2048)) ** 3).astype(np.int64); e = np.minimum(e, slot)
    lo = np.maximum(e, 7); w = np.minimum(lo + np.floor((2048 - lo) * rng.random((N, 8, 2048)) ** 4).astype(np.int64), 2047)
    m = 2048 * w + slot - e
    b = np.minimum(np.floor(256 * rng.random((N, 8, Q)) ** 6), 255)
    return {"states": some_states(rng), "models": m.astype(np.int32), "letters": rng.integers(0, 256, (N, 8, 2048)).astype(np.int32), "stock": b.astype(np.int32), "places": some_places(rng)}
def check_inputs(d):
    x, t, a, b, p = d["states"], d["models"].astype(np.int64), d["letters"], d["stock"], d["places"]; bad = []; slot = np.arange(2048)
    if not ((x >= 4096) & (x < 1048576)).all(): bad.append("states")
    if not ((t >= 14336) & (t < 4194304) & ((t & 2047) <= slot) & (slot <= (t & 2047) + (t >> 11))).all(): bad.append("models")
    if not ((a >= 0) & (a < 256)).all(): bad.append("letters")
    if not ((b >= 0) & (b < 256)).all(): bad.append("stock")
    if not ((np.sort(p, axis=2) == np.arange(N * Q)).all() and (p == p[:1]).all()): bad.append("places")
    return bad
def whole(b):
    return np.ascontiguousarray(b.transpose(1, 0, 2)).reshape(8, -1)
def line(v, s):
    return np.ascontiguousarray(v.transpose(1, 0, 2)).reshape(8, -1)
def unline(u, s):
    return u.reshape(8, N, L).transpose(1, 0, 2)
def reference(states, models, letters, stock, places):
    x = states.astype(np.int64); t = models.astype(np.int64); pool = whole(stock.astype(np.int64)); seq = places[0].astype(np.int64)
    syms = np.zeros((N, 8, S * L), np.int32); used = np.zeros(8, np.int64)
    for s in range(S):
        slot = x & 2047; e = np.take_along_axis(t, slot, 2)
        syms[:, :, s * L:(s + 1) * L] = np.take_along_axis(letters, slot, 2)
        x = ((e >> 11) + 1) * (x >> 11) + slot - (e & 2047)
        reads = x < 4096; w = line(reads, s).astype(np.int64)
        at = used[:, None] + np.add.accumulate(w, axis=1) - w
        x = np.where(reads, 256 * x + unline(np.take_along_axis(pool, np.take_along_axis(seq, at, 1), 1), s), x)
        used = used + np.add.reduce(w, axis=1)
    return {"syms": np.asarray(syms, np.float32), "last": np.asarray(x, np.float32)}

@@ -1,0 +1,324 @@
+import numpy as np
+from concourse.bass import DstId, RemoteDMATransfer
+from concourse.mybir import dt, AluOpType, AxisListType, ActivationFunctionType
+
+N, S, PAD, BIG = 8, 4, 16, 20000
+
+SCRATCH = {
+    "pS": ("dram", [8, 128, 2], "int32"), "pA": ("dram", [8, 128, 16], "int32"),
+    "pB": ("dram", [8, 128, 8], "bfloat16"), "pC": ("dram", [8, 128, 16], "bfloat16"),
+    "lS": ("dram", [8, 128, 2], "int32"), "lA": ("dram", [8, 128, 16], "int32"),
+    "lB": ("dram", [8, 128, 8], "bfloat16"), "lC": ("dram", [8, 128, 16], "bfloat16"),
+    "rY": ("dram", [8, 128, 4], "float32"), "rZ": ("dram", [8, 128, 2], "float32"), "rF": ("dram", [8, 128, 4], "float32"),
+    "lY": ("dram", [8, 128, 4], "float32"), "lZ": ("dram", [8, 128, 2], "float32"), "lF": ("dram", [8, 128, 4], "float32"),
+    "MW": ("sbuf", [128, 2048], "int32"), "PW": ("sbuf", [128, 8192], "bfloat16"),
+    "LW": ("sbuf", [128, 2048], "bfloat16"), "SQ": ("sbuf", [128, PAD + 8192], "bfloat16"),
+    "BI": ("sbuf", [128, 128], "int32"), "BF": ("sbuf", [128, 128], "float32"), "OW": ("sbuf", [128, 64], "uint16"),
+    "GB": ("sbuf", [128, 1024], "bfloat16"),
+    "IT": ("sbuf", [128, 272], "int32"), "IA": ("sbuf", [128, 272], "int32"),
+    "MK": ("sbuf", [128, 256], "float32"), "K16": ("sbuf", [128, 256], "float32"),
+    "ON": ("sbuf", [128, 128], "bfloat16"), "SU": ("sbuf", [128, 128], "bfloat16"), "ES": ("sbuf", [128, 144], "bfloat16"),
+    "ID": ("sbuf", [128, 128], "float32"), "CS": ("sbuf", [128, 8], "float32"), "SK": ("sbuf", [128, 1024], "bfloat16"),
+    "X0": ("sbuf", [128, 16], "int32"), "L0": ("sbuf", [128, 16], "int32"),
+    "OF": ("sbuf", [128, 64], "uint16"), "OT": ("sbuf", [128, 64], "uint16"),
+    "HI": ("sbuf", [128, 64], "int32"), "HH": ("sbuf", [128, 64], "float32"), "SL": ("sbuf", [128, 64], "float32"),
+    "AA": ("sbuf", [128, 64], "float32"), "A4": ("sbuf", [128, 64], "float32"), "FF": ("sbuf", [128, 64], "int32"),
+    "Q4": ("sbuf", [128, 64], "float32"), "QQ": ("sbuf", [128, 64], "float32"), "PP": ("sbuf", [128, 64], "float32"),
+    "RR": ("sbuf", [128, 64], "bfloat16"), "II": ("sbuf", [128, 64], "bfloat16"), "XX": ("sbuf", [128, 64], "float32"),
+    "MM": ("sbuf", [128, 64], "float32"), "NB": ("sbuf", [128, 64], "float32"), "VV": ("sbuf", [128, 64], "float32"),
+    "NH": ("sbuf", [128, 64], "float32"), "DD": ("sbuf", [128, 64], "float32"),
+    "I2": ("sbuf", [128, 64], "float32"), "SY": ("sbuf", [128, 64], "float32"), "FN": ("sbuf", [128, 16], "float32"),
+    "PR0": ("psum", [128, 512], "float32"), "PR1": ("psum", [128, 512], "float32"), "CP": ("psum", [128, 512], "float32"),
+}
+for _s in range(S):
+    SCRATCH["MA%d" % _s] = ("sbuf", [128, 256], "float32")
+    SCRATCH["SA%d" % _s] = ("sbuf", [128, 256], "float32")
+    SCRATCH["MB%d" % _s] = ("sbuf", [128, 256], "float32")
+    SCRATCH["SB%d" % _s] = ("sbuf", [128, 256], "float32")
+    SCRATCH["LG%d" % _s] = ("sbuf", [128, 256], "bfloat16")
+for _b in range(5):
+    SCRATCH["QB%d" % _b] = ("psum", [128, 512], "float32")
+
+SEMAPHORES = (["aS", "aA", "aB", "aC", "aY", "aZ", "aF", "sent"]
+              + ["gB", "gC", "dS", "dA", "oS", "oA", "oB", "oC", "dPl", "dX", "dPW", "dMWa", "dMWb", "dLW"]
+              + ["dY", "dZ", "dF3", "dFl", "oY", "oZ", "oF3", "oFl", "out1", "out2"]
+              + ["mPW", "mLW", "it", "ia", "mk", "k16", "k16b", "on", "su", "es", "id", "cs", "sk", "pad",
+                 "bf", "tp", "ow", "gp0", "gp1", "gp2"]
+              + ["sq%d" % j for j in range(16)] + ["cp%d" % j for j in range(16)]
+              + ["lo", "hi", "hh", "of", "sl", "ga", "aa", "a4", "sa", "ff", "q4", "pp", "qq", "rr", "ii", "pf", "xx", "m2", "nb",
+                 "vv", "nh", "i2", "ot", "gb", "dd", "sb", "fn", "lg", "lc", "sy"])
+
+
+def rank_program(g, core, T, topo):
+    me = T.rank_of(core)
+    if me is None:
+        return
+    A, AF = AluOpType, ActivationFunctionType
+    V, C, TE, Y = g.vector, g.scalar, g.tensor, g.sync
+    count, known, seen = {}, {}, {}
+
+    def fire(ins, name, n=1):
+        ins.then_inc(T.sem[name], n)
+        count[name] = count.get(name, 0) + n
+        return (name, count[name])
+
+    def wait(q, *tokens):
+        for name, val in tokens:
+            k = (q[0], name)
+            if known.get(k, 0) < val:
+                known[k] = val
+                seen[name] = max(seen.get(name, 0), val)
+                q[1].wait_ge(T.sem[name], val)
+
+    qg, qv, qc, qt, qy = ("g", g), ("v", V), ("c", C), ("t", TE), ("y", Y)
+
+    engine = {}
+    for d in T.cores:
+        if d != core and topo.chip(d) != topo.chip(core):
+            e = topo.engines(core, d)
+            engine[d] = [x for x in e[0::2] + e[1::2] if x not in engine.values()][0]
+    for d in T.cores:
+        if d != core and topo.chip(d) == topo.chip(core):
+            engine[d] = [x for x in topo.engines(core, d)[::-1] if x not in engine.values()][0]
+
+    def send(src, dst, sem):
+        tr = []
+        for d in engine:
+            rid, pid, _ = topo.addr(d)
+            tr.append(RemoteDMATransfer(dst_ids=[DstId(rid=rid, pnc=pid)], dma_engine_mask=1 << engine[d], remote_sem=T.sem[sem],
+                                        srcs=[T[src][T.rank_of(d)]], dsts=[T[dst][me]], alu_op=0))
+        g.remote_dma_fused(tr, local_sem=T.sem.sent)
+        count["sent"] = count.get("sent", 0) + len(tr)
+        count[sem] = count.get(sem, 0) + len(tr)
+        return (sem, len(tr))
+
+    tdS = fire(Y.dma_start(T.pS[:], T.states[:]), "dS", 16)
+    tdA = fire(Y.dma_start(T.pA[:], T.models[:]), "dA", 16)
+    tgB = fire(g.dma_start(T.pB[:], T.stock[:]), "gB", 16)
+    tgC = fire(g.dma_start(T.pC[:], T.letters[:]), "gC", 16)
+    toS = fire(C.dma_start(T.lS[me], T.states[me]), "oS", 16)
+    toA = fire(C.dma_start(T.lA[me], T.models[me]), "oA", 16)
+    for h in range(2):
+        for k in range(8):
+            t = 4096 * h + 512 * k
+            tPl = fire((Y if h == 0 else C).dma_start(T.BI[32 * h:32 * h + 32, 16 * k:16 * k + 16], T.places[me, t:t + 512]), "dPl", 16)
+    tit = fire(g.iota(T.IT[:], [[1, 272]], -15, -1), "it")
+    wait(qg, tdS)
+    aS = send("pS", "lS", "aS")
+    wait(qg, tdA)
+    aA = send("pA", "lA", "aA")
+    wait(qg, tgB)
+    aB = send("pB", "lB", "aB")
+    wait(qg, tgC)
+    aC = send("pC", "lC", "aC")
+
+    tmPW = fire(V.memset(T.PW[:], 0.0), "mPW")
+    wait(qv, tit)
+    tid = fire(V.tensor_scalar(T.ID[:], T.IT[:, 15:143], 0, None, A.is_equal), "id")
+    wait(qv, tPl)
+    tbf = fire(V.tensor_copy(T.BF[0:64, :], T.BI[0:64, :]), "bf")
+    ton = fire(V.memset(T.ON[:], 1.0), "on")
+    tcs = fire(V.tensor_scalar(T.CS[:], T.IT[:, 15:143:16], 0, None, A.is_equal), "cs")
+    tsu = fire(V.tensor_scalar(T.SU[:], T.IT[:, 15:143], 0, None, A.is_gt), "su")
+    tia = fire(V.tensor_scalar(T.IA[:], T.IT[:], 15, None, A.bitwise_and), "ia")
+    tpad = fire(V.memset(T.SQ[:, 0:PAD], 0.0), "pad")
+    tk6 = fire(V.memset(T.K16[:], 1.0), "k16")
+    wait(qv, tia)
+    tmk = fire(V.tensor_scalar(T.MK[:], T.IA[:, 15:271], 0, None, A.is_equal), "mk")
+    wait(qv, tk6, tmk)
+    tk6b = fire(V.memset(T.K16[:, 0:256:16], 0.0), "k16b")
+    tes = fire(V.tensor_scalar(T.ES[:], T.IT[:, 0:144], 0, T.MK[:, 0:1], A.is_equal, A.mult), "es")
+    wait(qt, tid, tbf)
+    ttp = fire(TE.transpose(T.CP[:, 64:128], T.BF[0:64, :], T.ID[0:64, 0:64]), "tp")
+    wait(qv, ttp)
+    tow = fire(V.tensor_copy(T.OW[:], T.CP[:, 64:128]), "ow")
+    tmLW = fire(V.memset(T.LW[:], 0.0), "mLW")
+    wait(qc, ton, tcs)
+    for k in range(8):
+        tsk = fire(C.activation(T.SK[:, 128 * k:128 * k + 128], T.ON[:], AF.Copy, scale=T.CS[:, k:k + 1]), "sk")
+
+    wait(qy, tgB)
+    toB = fire(Y.dma_start(T.lB[me], T.pB[me]), "oB", 16)
+    wait(qy, aS, toS)
+    tX = fire(Y.dma_start(T.X0[:], T.lS[:]), "dX", 16)
+    wait(qy, aA, toA)
+    for q in range(8):
+        tMa = fire(Y.dma_start(T.MW[q:128:16, :], T.lA[:]), "dMWa", 16)
+    wait(qc, aA, toA)
+    for q in range(8, 16):
+        tMb = fire(C.dma_start(T.MW[q:128:16, :], T.lA[:]), "dMWb", 16)
+    wait(qy, aB, toB, tmPW)
+    for k in range(8):
+        tPW = fire(Y.dma_start(T.PW[16 * k:16 * k + 1, :], T.lB[:]), "dPW", 16)
+    wait(qy, tgC)
+    toC = fire(Y.dma_start(T.lC[me], T.pC[me]), "oC", 16)
+    wait(qy, aC, toC, tmLW)
+    tLW = fire(Y.dma_start(T.LW[0:128:16, :], T.lC[:]), "dLW", 16)
+
+    wait(qv, tX)
+    tlo = fire(V.tensor_scalar(T.L0[:], T.X0[:], 2047, None, A.bitwise_and), "lo")
+    thi = fire(V.tensor_scalar(T.HI[:, 0:16], T.X0[:], 11, None, A.arith_shift_right), "hi")
+    wait(qv, tlo)
+    tof = fire(V.tensor_copy(T.OF[:, 0:16], T.L0[:]), "of")
+    tsl = fire(V.tensor_copy(T.SL[:, 0:16], T.L0[:]), "sl")
+    wait(qv, thi)
+    thh = fire(V.tensor_scalar(T.HH[:, 0:16], T.HI[:, 0:16], 2048, None, A.add), "hh")
+    wait(qv, tow, tPW)
+    tg0 = fire(V.tensor_copy(T.GB[:, 0:256], T.PW[:].indirect(T.OW[:, 0:16])), "gp0")
+    wait(qc, tow, tPW)
+    tg1 = fire(C.activation(T.GB[:, 256:512], T.PW[:].indirect(T.OW[:, 16:32]), AF.Copy), "gp1")
+
+    tcp, tsq = {}, {}
+
+    def seq(j):
+        wait(qt, tsk, tg0, tg1)
+        if j >= 8:
+            wait(qt, tg2)
+        if j >= 5:
+            wait(qt, tcp[j - 5])
+        k, h = j % 8, j // 8
+        tsq[j] = fire(TE.matmul(T["QB%d" % (j % 5)][:], T.SK[:, 128 * k:128 * k + 128], T.GB[:, 512 * h:512 * h + 512], True, True), "sq%d" % j)
+
+    def cpy(j, q):
+        wait(q, tsq[j])
+        out, in_ = T.SQ[:, PAD + 512 * j:PAD + 512 * j + 512], T["QB%d" % (j % 5)][:]
+        tcp[j] = fire(C.activation(out, in_, AF.Copy) if q is qc else V.tensor_copy(out, in_), "cp%d" % j)
+
+    for j in range(4):
+        seq(j)
+        cpy(j, qc if j % 2 == 0 else qv)
+    tg2 = fire(C.activation(T.GB[:, 512:1024], T.PW[:].indirect(T.OW[:, 32:64]), AF.Copy), "gp2")
+    seq(4)
+
+    tlg, tlc, tsy, tii = {}, {}, {}, {}
+
+    def letters(s, tok):
+        wait(qc, tok, tLW)
+        tlg[s] = fire(C.activation(T["LG%d" % s][:], T.LW[:].indirect(T.OF[:, 16 * s:16 * s + 16]), AF.Copy), "lg")
+
+    def compact(s):
+        wait(qt, tlg[s], tes, tow)
+        if s:
+            wait(qt, tsy[s - 1])
+        for q in range(16):
+            m = TE.matmul(T.CP[:, 16 * s:16 * s + 16], T.ES[:, 15 - q:143 - q], T["LG%d" % s][:, q:256:16], q == 0, q == 15)
+        tlc[s] = fire(m, "lc")
+        wait(qc, tlc[s])
+        tsy[s] = fire(C.activation(T.SY[:, 16 * s:16 * s + 16], T.CP[:, 16 * s:16 * s + 16], AF.Copy), "sy")
+
+    toff = {0: tof}
+    for s in range(S):
+        c = slice(16 * s, 16 * s + 16)
+        n = slice(16 * s + 16, 16 * s + 32)
+        MA, SA, MB, SB = T["MA%d" % s], T["SA%d" % s], T["MB%d" % s], T["SB%d" % s]
+        if s == 0:
+            wait(qv, tMa, tMb, tmk)
+        wait(qv, toff[s])
+        tga = fire(V.tensor_tensor(MA[:], T.MW[:].indirect(T.OF[:, c]), T.MK[:], A.mult), "ga")
+        wait(qv, tsl)
+        taa = fire(V.tensor_tensor(T.AA[:, c], T.HI[:, c], T.SL[:, c], A.add), "aa")
+        wait(qv, tga, tk6b)
+        tsa = fire(V.tensor_tensor_scan(SA[:], T.K16[:], MA[:], 0.0, A.mult, A.add), "sa")
+        wait(qv, taa)
+        ta4 = fire(V.tensor_scalar(T.A4[:, c], T.AA[:, c], -4096, None, A.add), "a4")
+        wait(qv, tsa)
+        e = SA[:, 15:256:16]
+        tff = fire(V.tensor_scalar(T.FF[:, c], e, 1.0 / 2048, -1023.5 / 2048, A.mult, A.add), "ff")
+        wait(qv, ta4)
+        tq4 = fire(V.tensor_tensor(T.Q4[:, c], e, T.A4[:, c], A.subtract), "q4")
+        wait(qv, tff, thh)
+        tpp = fire(V.tensor_tensor(T.PP[:, c], T.FF[:, c], T.HH[:, c], A.mult), "pp")
+        tqq = fire(V.tensor_tensor(T.QQ[:, c], T.AA[:, c], e, A.subtract), "qq")
+        wait(qv, tpp, tq4)
+        trr = fire(V.tensor_tensor(T.RR[:, c], T.PP[:, c], T.Q4[:, c], A.is_lt), "rr")
+        wait(qv, tqq)
+        txx = fire(V.tensor_tensor(T.XX[:, c], T.PP[:, c], T.QQ[:, c], A.add), "xx")
+        wait(qv, trr, ton)
+        tii[s] = fire(V.tensor_tensor_scan(T.II[:, c], T.ON[:, 0:16], T.RR[:, c], 0.0, A.mult, A.add), "ii")
+        tm2 = fire(V.tensor_scalar(T.MM[:, c], T.RR[:, c], 255, 1, A.mult, A.add), "m2")
+        tnb = fire(V.tensor_scalar(T.NB[:, c], T.RR[:, c], BIG, PAD - 1 - BIG, A.mult, A.add), "nb")
+        PR = T["PR%d" % (s % 2)]
+        wait(qt, tsu)
+        if s:
+            wait(qt, tii[s - 1])
+        for b in range(s):
+            TE.matmul(PR[:, s:s + 1], T.ON[:], T.II[:, 16 * b + 15:16 * b + 16], b == 0, False)
+        wait(qt, tii[s])
+        tpf = fire(TE.matmul(PR[:, s:s + 1], T.SU[:], T.II[:, 16 * s + 15:16 * s + 16], s == 0, True), "pf")
+        if s == 0:
+            for j in range(4, 8):
+                if j > 4:
+                    seq(j)
+                cpy(j, qc)
+        else:
+            compact(s - 1)
+            if s < 3:
+                for j in range(4 * s + 4, 4 * s + 8):
+                    seq(j)
+                    cpy(j, qc)
+        letters(s, toff[s])
+        wait(qv, tm2, txx)
+        tvv = fire(V.tensor_tensor(T.VV[:, c], T.XX[:, c], T.MM[:, c], A.mult), "vv")
+        wait(qv, tnb, tii[s])
+        ti2 = fire(V.tensor_tensor(T.I2[:, c], T.II[:, c], T.NB[:, c], A.add), "i2")
+        if s < 3:
+            wait(qv, tvv)
+            thi = fire(V.tensor_scalar(T.HI[:, n], T.VV[:, c], 1.0 / 2048, -1023.5 / 2048, A.mult, A.add), "hi")
+        wait(qv, ti2, tpf)
+        tot = fire(V.tensor_scalar(T.OT[:, c], T.I2[:, c], PR[:, s:s + 1], None, A.add), "ot")
+        wait(qv, tot, tpad, *[tcp[j] for j in range(4 * s + 4)])
+        tgb = fire(V.tensor_tensor(MB[:], T.SQ[:, 0:PAD + 2048 * (s + 1)].indirect(T.OT[:, c]), T.MK[:], A.mult), "gb")
+        if s < 3:
+            wait(qv, thi)
+            tnh = fire(V.tensor_scalar(T.NH[:, c], T.HI[:, n], -2048, None, A.mult), "nh")
+            thh = fire(V.tensor_scalar(T.HH[:, n], T.HI[:, n], 2048, None, A.add), "hh")
+        wait(qv, tgb)
+        tsb = fire(V.tensor_tensor_scan(SB[:], T.K16[:], MB[:], 0.0, A.mult, A.add), "sb")
+        b = SB[:, 15:256:16]
+        if s < 3:
+            wait(qv, tnh)
+            tdd = fire(V.tensor_tensor(T.DD[:, c], T.VV[:, c], T.NH[:, c], A.add), "dd")
+            wait(qv, tsb, tdd)
+            tsl = fire(V.tensor_tensor(T.SL[:, n], b, T.DD[:, c], A.add), "sl")
+            wait(qv, tsl)
+            toff[s + 1] = fire(V.tensor_copy(T.OF[:, n], T.SL[:, n]), "of")
+        else:
+            wait(qv, tsb, tvv)
+            tfn = fire(V.tensor_tensor(T.FN[:], b, T.VV[:, c], A.add), "fn")
+    compact(3)
+
+    m0 = slice(16 * me, 16 * me + 16)
+    half = {0: slice(0, 64), 1: slice(64, 128), 2: slice(0, 128), 3: slice(0, 64)}
+
+    def put(s, out, own, so, sw):
+        wait(qy, tsy[s])
+        c = slice(16 * s, 16 * s + 16)
+        a = fire(Y.dma_start(out[:, half[s], :], T.SY[:, c]), so, 16)
+        b = fire(Y.dma_start(own[me, half[s], :], T.SY[m0, c]), sw, 16)
+        return a, b
+
+    put(0, T.rY, T.lY, "dY", "oY")
+    a, oY = put(1, T.rY, T.lY, "dY", "oY")
+    wait(qg, a)
+    aY = send("rY", "lY", "aY")
+    a, oZ = put(2, T.rZ, T.lZ, "dZ", "oZ")
+    wait(qg, a)
+    aZ = send("rZ", "lZ", "aZ")
+    a, oF3 = put(3, T.rF, T.lF, "dF3", "oF3")
+    wait(qy, tfn)
+    b = fire(Y.dma_start(T.rF[:, 64:128, :], T.FN[:]), "dFl", 16)
+    wait(qc, tfn)
+    oFl = fire(C.dma_start(T.lF[me, 64:128, :], T.FN[m0, :]), "oFl", 16)
+    wait(qg, a, b)
+    aF = send("rF", "lF", "aF")
+    wait(qc, aY, oY)
+    fire(C.dma_start(T.syms[:, 0:512], T.lY[:]), "out2", 16)
+    wait(qc, aZ, oZ)
+    fire(C.dma_start(T.syms[:, 512:768], T.lZ[:]), "out2", 16)
+    wait(qy, aF, oFl)
+    fire(Y.dma_start(T.last[:], T.lF[:, 64:128, :]), "out1", 16)
+    wait(qc, aF, oF3)
+    fire(C.dma_start(T.syms[:, 768:1024], T.lF[:, 0:64, :]), "out2", 16)
+    for name in count:
+        if seen.get(name, 0) < count[name]:
+            wait(qg, (name, count[name]))

@@ -6,17 +6,22 @@ N, S, PAD, BIG = 8, 4, 16, 20000
 
 SCRATCH = {
     "pS": ("dram", [8, 128, 2], "int32"), "pA": ("dram", [8, 128, 16], "int32"),
-    "pB": ("dram", [8, 128, 8], "bfloat16"), "pC": ("dram", [8, 128, 16], "bfloat16"),
+    "pB": ("dram", [8, 128, 8], "int32"), "pC": ("dram", [8, 128, 16], "bfloat16"),
     "lS": ("dram", [8, 128, 2], "int32"), "lA": ("dram", [8, 128, 16], "int32"),
-    "lB": ("dram", [8, 128, 8], "bfloat16"), "lC": ("dram", [8, 128, 16], "bfloat16"),
+    "lB": ("dram", [8, 128, 8], "int32"), "lC": ("dram", [8, 128, 16], "bfloat16"),
     "rY": ("dram", [8, 128, 4], "float32"), "rZ": ("dram", [8, 128, 2], "float32"), "rF": ("dram", [8, 128, 4], "float32"),
     "lY": ("dram", [8, 128, 4], "float32"), "lZ": ("dram", [8, 128, 2], "float32"), "lF": ("dram", [8, 128, 4], "float32"),
-    "MW": ("sbuf", [128, 2048], "int32"), "PW": ("sbuf", [128, 8192], "bfloat16"),
+    "CW": ("sbuf", [128, 128], "int32"), "CN": ("sbuf", [128, 128], "bfloat16"),
+    "MW": ("sbuf", [128, 2048], "int32"), "PW": ("sbuf", [128, 512], "int32"),
     "LW": ("sbuf", [128, 2048], "bfloat16"), "SQ": ("sbuf", [128, PAD + 8192], "bfloat16"),
-    "BI": ("sbuf", [128, 128], "int32"), "BF": ("sbuf", [128, 128], "float32"), "OW": ("sbuf", [128, 64], "uint16"),
-    "GB": ("sbuf", [128, 1024], "bfloat16"),
-    "IT": ("sbuf", [128, 272], "int32"), "IA": ("sbuf", [128, 272], "int32"),
-    "MK": ("sbuf", [128, 256], "float32"), "K16": ("sbuf", [128, 256], "float32"),
+    "BI": ("sbuf", [128, 128], "int32"), "BJ": ("sbuf", [128, 128], "int32"), "BF": ("sbuf", [128, 128], "float32"),
+    "OW": ("sbuf", [128, 64], "uint16"), "P8": ("sbuf", [128, 1024], "int32"), "P9": ("sbuf", [128, 1024], "int32"),
+    "PB": ("sbuf", [128, 1024], "bfloat16"), "ZM": ("sbuf", [128, 1024], "bfloat16"), "GB": ("sbuf", [128, 1024], "bfloat16"),
+    "IT": ("sbuf", [128, 272], "int32"), "IA": ("sbuf", [128, 272], "int32"), "QI": ("sbuf", [128, 8], "int32"),
+    "KI": ("sbuf", [128, 8], "int32"), "GI": ("sbuf", [128, 128], "int32"), "GS": ("sbuf", [128, 128], "bfloat16"),
+    "QA": ("sbuf", [128, 8], "int32"), "QD": ("sbuf", [128, 8], "int32"), "QF": ("sbuf", [128, 8], "float32"),
+    "PF": ("sbuf", [128, 8], "float32"),
+    "MK": ("sbuf", [128, 256], "float32"), "K16": ("sbuf", [128, 256], "float32"), "KB": ("sbuf", [128, 256], "bfloat16"),
     "ON": ("sbuf", [128, 128], "bfloat16"), "SU": ("sbuf", [128, 128], "bfloat16"), "ES": ("sbuf", [128, 144], "bfloat16"),
     "ID": ("sbuf", [128, 128], "float32"), "CS": ("sbuf", [128, 8], "float32"), "SK": ("sbuf", [128, 1024], "bfloat16"),
     "X0": ("sbuf", [128, 16], "int32"), "L0": ("sbuf", [128, 16], "int32"),
@@ -33,17 +38,18 @@ SCRATCH = {
 for _s in range(S):
     SCRATCH["MA%d" % _s] = ("sbuf", [128, 256], "float32")
     SCRATCH["SA%d" % _s] = ("sbuf", [128, 256], "float32")
-    SCRATCH["MB%d" % _s] = ("sbuf", [128, 256], "float32")
-    SCRATCH["SB%d" % _s] = ("sbuf", [128, 256], "float32")
+    SCRATCH["MB%d" % _s] = ("sbuf", [128, 256], "bfloat16")
+    SCRATCH["SB%d" % _s] = ("sbuf", [128, 256], "bfloat16")
     SCRATCH["LG%d" % _s] = ("sbuf", [128, 256], "bfloat16")
 for _b in range(5):
     SCRATCH["QB%d" % _b] = ("psum", [128, 512], "float32")
 
 SEMAPHORES = (["aS", "aA", "aB", "aC", "aY", "aZ", "aF", "sent"]
-              + ["gB", "gC", "dS", "dA", "oS", "oA", "oB", "oC", "dPl", "dX", "dPW", "dMWa", "dMWb", "dLW"]
+              + ["dB", "dC", "wC", "nC", "dS", "dA", "oS", "oA", "oB", "oC", "dPl", "dP8", "dX", "dPW", "dMWa", "dMWb", "dLW"]
               + ["dY", "dZ", "dF3", "dFl", "oY", "oZ", "oF3", "oFl", "out1", "out2"]
-              + ["mPW", "mLW", "it", "ia", "mk", "k16", "k16b", "on", "su", "es", "id", "cs", "sk", "pad",
-                 "bf", "tp", "ow", "gp0", "gp1", "gp2"]
+              + ["mLW", "it", "qi", "ki", "gi", "gs", "qa", "qd", "qf", "pF", "p9", "pb", "zt", "zm0", "zm1",
+                 "ia", "mk", "k16", "k16b", "kb", "kbb", "on", "su", "es", "id", "cs", "sk", "pad",
+                 "bj", "bf", "tp", "ow", "gp0", "gp1"]
               + ["sq%d" % j for j in range(16)] + ["cp%d" % j for j in range(16)]
               + ["lo", "hi", "hh", "of", "sl", "ga", "aa", "a4", "sa", "ff", "q4", "pp", "qq", "rr", "ii", "pf", "xx", "m2", "nb",
                  "vv", "nh", "i2", "ot", "gb", "dd", "sb", "fn", "lg", "lc", "sy"])
@@ -92,69 +98,100 @@ def rank_program(g, core, T, topo):
         count[sem] = count.get(sem, 0) + len(tr)
         return (sem, len(tr))
 
-    tdS = fire(Y.dma_start(T.pS[:], T.states[:]), "dS", 16)
+    m0 = slice(16 * me, 16 * me + 16)
     tdA = fire(Y.dma_start(T.pA[:], T.models[:]), "dA", 16)
-    tgB = fire(g.dma_start(T.pB[:], T.stock[:]), "gB", 16)
-    tgC = fire(g.dma_start(T.pC[:], T.letters[:]), "gC", 16)
-    toS = fire(C.dma_start(T.lS[me], T.states[me]), "oS", 16)
+    tdB = fire(C.dma_start(T.pB[:], T.stock[:]), "dB", 16)
+    tdS = fire(Y.dma_start(T.pS[:], T.states[:]), "dS", 16)
+    twC = fire(C.dma_start(T.CW[:], T.letters[:]), "wC", 16)
+    tP8 = fire(Y.dma_start(T.P8[0:8, :], T.places[me]), "dP8", 16)
     toA = fire(C.dma_start(T.lA[me], T.models[me]), "oA", 16)
-    for h in range(2):
-        for k in range(8):
-            t = 4096 * h + 512 * k
-            tPl = fire((Y if h == 0 else C).dma_start(T.BI[32 * h:32 * h + 32, 16 * k:16 * k + 16], T.places[me, t:t + 512]), "dPl", 16)
+    toS = fire(Y.dma_start(T.lS[me], T.states[me]), "oS", 16)
+    toB = fire(C.dma_start(T.lB[me], T.stock[me]), "oB", 16)
+    for k in range(8):
+        tPl = fire((Y if k % 2 else C).dma_start(T.BI[0:64, 16 * k:16 * k + 16], T.places[me, 1024 * k:1024 * k + 1024]), "dPl", 16)
     tit = fire(g.iota(T.IT[:], [[1, 272]], -15, -1), "it")
-    wait(qg, tdS)
-    aS = send("pS", "lS", "aS")
+    tgi = fire(g.iota(T.GI[0:8, :], [[1, 8], [0, 16]], 0, -1), "gi")
+    tqi = fire(g.iota(T.QI[:], [[0, 8]], 0, 1), "qi")
+    tki = fire(g.iota(T.KI[:], [[1, 8]], 0, 0), "ki")
     wait(qg, tdA)
     aA = send("pA", "lA", "aA")
-    wait(qg, tgB)
+    wait(qg, tdB)
     aB = send("pB", "lB", "aB")
-    wait(qg, tgC)
-    aC = send("pC", "lC", "aC")
+    wait(qg, tdS)
+    aS = send("pS", "lS", "aS")
 
-    tmPW = fire(V.memset(T.PW[:], 0.0), "mPW")
-    wait(qv, tit)
-    tid = fire(V.tensor_scalar(T.ID[:], T.IT[:, 15:143], 0, None, A.is_equal), "id")
-    wait(qv, tPl)
-    tbf = fire(V.tensor_copy(T.BF[0:64, :], T.BI[0:64, :]), "bf")
     ton = fire(V.memset(T.ON[:], 1.0), "on")
-    tcs = fire(V.tensor_scalar(T.CS[:], T.IT[:, 15:143:16], 0, None, A.is_equal), "cs")
-    tsu = fire(V.tensor_scalar(T.SU[:], T.IT[:, 15:143], 0, None, A.is_gt), "su")
-    tia = fire(V.tensor_scalar(T.IA[:], T.IT[:], 15, None, A.bitwise_and), "ia")
-    tpad = fire(V.memset(T.SQ[:, 0:PAD], 0.0), "pad")
     tk6 = fire(V.memset(T.K16[:], 1.0), "k16")
+    tkb = fire(V.memset(T.KB[:], 1.0), "kb")
+    wait(qv, tit)
+    tia = fire(V.tensor_scalar(T.IA[:], T.IT[:], 15, None, A.bitwise_and), "ia")
+    tid = fire(V.tensor_scalar(T.ID[:], T.IT[:, 15:143], 0, None, A.is_equal), "id")
+    tsu = fire(V.tensor_scalar(T.SU[:], T.IT[:, 15:143], 0, None, A.is_gt), "su")
     wait(qv, tia)
     tmk = fire(V.tensor_scalar(T.MK[:], T.IA[:, 15:271], 0, None, A.is_equal), "mk")
-    wait(qv, tk6, tmk)
+    wait(qv, tk6, tkb)
     tk6b = fire(V.memset(T.K16[:, 0:256:16], 0.0), "k16b")
+    tkbb = fire(V.memset(T.KB[:, 0:256:16], 0.0), "kbb")
+    wait(qv, tgi, tqi, tki)
+    tgs = fire(V.tensor_scalar(T.GS[0:8, :], T.GI[0:8, :], 0, None, A.is_equal), "gs")
+    tqa = fire(V.tensor_scalar(T.QA[:], T.QI[:], 15, None, A.bitwise_and), "qa")
+    tqd = fire(V.tensor_scalar(T.QD[:], T.QI[:], 4, None, A.arith_shift_right), "qd")
+    wait(qv, tqa)
+    tqf = fire(V.tensor_copy(T.QF[:], T.QA[:]), "qf")
+    wait(qv, tqd)
+    tpF = fire(V.tensor_copy(T.PF[:], T.QD[:]), "pF")
+    wait(qv, tpF)
+    tcs = fire(V.tensor_scalar(T.CS[:], T.KI[:], T.PF[:, 0:1], None, A.is_equal), "cs")
+    wait(qv, tP8)
+    tp9 = fire(V.tensor_scalar(T.P9[0:8, :], T.P8[0:8, :], 9, None, A.arith_shift_right), "p9")
+    wait(qv, twC)
+    tnC = fire(V.tensor_copy(T.CN[:], T.CW[:]), "nC")
+    wait(qv, tp9)
+    tpb = fire(V.tensor_copy(T.PB[0:8, :], T.P9[0:8, :]), "pb")
+    wait(qv, tPl)
+    tbj = fire(V.tensor_scalar(T.BJ[0:64, :], T.BI[0:64, :], 511, None, A.bitwise_and), "bj")
+    wait(qv, tmk)
     tes = fire(V.tensor_scalar(T.ES[:], T.IT[:, 0:144], 0, T.MK[:, 0:1], A.is_equal, A.mult), "es")
+    wait(qv, tbj)
+    tbf = fire(V.tensor_copy(T.BF[0:64, :], T.BJ[0:64, :]), "bf")
+    tpad = fire(V.memset(T.SQ[:, 0:PAD], 0.0), "pad")
+    wait(qt, tgs, tpb)
+    TE.matmul(T.QB0[:], T.GS[0:8, :], T.PB[0:8, 0:512], True, True)
+    tzt = fire(TE.matmul(T.QB1[:], T.GS[0:8, :], T.PB[0:8, 512:1024], True, True), "zt")
     wait(qt, tid, tbf)
     ttp = fire(TE.transpose(T.CP[:, 64:128], T.BF[0:64, :], T.ID[0:64, 0:64]), "tp")
+    wait(qv, tzt, tqf)
+    tz0 = fire(V.tensor_scalar(T.ZM[:, 0:512], T.QB0[:], T.QF[:, 0:1], None, A.is_equal), "zm0")
+    tz1 = fire(V.tensor_scalar(T.ZM[:, 512:1024], T.QB1[:], T.QF[:, 0:1], None, A.is_equal), "zm1")
     wait(qv, ttp)
     tow = fire(V.tensor_copy(T.OW[:], T.CP[:, 64:128]), "ow")
     tmLW = fire(V.memset(T.LW[:], 0.0), "mLW")
+
+    wait(qc, tnC)
+    tdC = fire(C.dma_start(T.pC[:], T.CN[:]), "dC", 16)
+    toC = fire(C.dma_start(T.lC[me], T.CN[m0, :]), "oC", 16)
+    wait(qg, tdC)
+    aC = send("pC", "lC", "aC")
+    wait(qc, aA, toA)
+    for q in range(8, 16):
+        tMb = fire(C.dma_start(T.MW[q:128:16, :], T.lA[:]), "dMWb", 16)
+    wait(qy, aB, toB)
+    for k in range(8):
+        tPW = fire(Y.dma_start(T.PW[16 * k:16 * k + 16, :], T.lB[:]), "dPW", 16)
+    wait(qy, aA, toA)
+    for q in range(8):
+        tMa = fire(Y.dma_start(T.MW[q:128:16, :], T.lA[:]), "dMWa", 16)
+    wait(qy, aS, toS)
+    tX = fire(Y.dma_start(T.X0[:], T.lS[:]), "dX", 16)
+    wait(qy, aC, toC, tmLW)
+    tLW = fire(Y.dma_start(T.LW[0:128:16, :], T.lC[:]), "dLW", 16)
     wait(qc, ton, tcs)
     for k in range(8):
         tsk = fire(C.activation(T.SK[:, 128 * k:128 * k + 128], T.ON[:], AF.Copy, scale=T.CS[:, k:k + 1]), "sk")
 
-    wait(qy, tgB)
-    toB = fire(Y.dma_start(T.lB[me], T.pB[me]), "oB", 16)
-    wait(qy, aS, toS)
-    tX = fire(Y.dma_start(T.X0[:], T.lS[:]), "dX", 16)
-    wait(qy, aA, toA)
-    for q in range(8):
-        tMa = fire(Y.dma_start(T.MW[q:128:16, :], T.lA[:]), "dMWa", 16)
-    wait(qc, aA, toA)
-    for q in range(8, 16):
-        tMb = fire(C.dma_start(T.MW[q:128:16, :], T.lA[:]), "dMWb", 16)
-    wait(qy, aB, toB, tmPW)
-    for k in range(8):
-        tPW = fire(Y.dma_start(T.PW[16 * k:16 * k + 1, :], T.lB[:]), "dPW", 16)
-    wait(qy, tgC)
-    toC = fire(Y.dma_start(T.lC[me], T.pC[me]), "oC", 16)
-    wait(qy, aC, toC, tmLW)
-    tLW = fire(Y.dma_start(T.LW[0:128:16, :], T.lC[:]), "dLW", 16)
-
+    wait(qv, tow, tz0, tz1, tPW)
+    tg0 = fire(V.tensor_tensor(T.GB[:, 0:512], T.PW[:].indirect(T.OW[:, 0:32]), T.ZM[:, 0:512], A.mult), "gp0")
+    tg1 = fire(V.tensor_tensor(T.GB[:, 512:1024], T.PW[:].indirect(T.OW[:, 32:64]), T.ZM[:, 512:1024], A.mult), "gp1")
     wait(qv, tX)
     tlo = fire(V.tensor_scalar(T.L0[:], T.X0[:], 2047, None, A.bitwise_and), "lo")
     thi = fire(V.tensor_scalar(T.HI[:, 0:16], T.X0[:], 11, None, A.arith_shift_right), "hi")
@@ -163,31 +200,27 @@ def rank_program(g, core, T, topo):
     tsl = fire(V.tensor_copy(T.SL[:, 0:16], T.L0[:]), "sl")
     wait(qv, thi)
     thh = fire(V.tensor_scalar(T.HH[:, 0:16], T.HI[:, 0:16], 2048, None, A.add), "hh")
-    wait(qv, tow, tPW)
-    tg0 = fire(V.tensor_copy(T.GB[:, 0:256], T.PW[:].indirect(T.OW[:, 0:16])), "gp0")
-    wait(qc, tow, tPW)
-    tg1 = fire(C.activation(T.GB[:, 256:512], T.PW[:].indirect(T.OW[:, 16:32]), AF.Copy), "gp1")
 
-    tcp, tsq = {}, {}
+    tcp, tsq, banks = {}, {}, []
 
     def seq(j):
-        wait(qt, tsk, tg0, tg1)
-        if j >= 8:
-            wait(qt, tg2)
-        if j >= 5:
-            wait(qt, tcp[j - 5])
-        k, h = j % 8, j // 8
-        tsq[j] = fire(TE.matmul(T["QB%d" % (j % 5)][:], T.SK[:, 128 * k:128 * k + 128], T.GB[:, 512 * h:512 * h + 512], True, True), "sq%d" % j)
+        wait(qt, tsk, tz0, tz1, tg1 if j % 2 else tg0)
+        n = len(banks)
+        if n >= 5:
+            wait(qt, tcp[banks[n - 5]])
+        banks.append(j)
+        k, h = j // 2, j % 2
+        tsq[j] = (n % 5, fire(TE.matmul(T["QB%d" % (n % 5)][:], T.SK[:, 128 * k:128 * k + 128], T.GB[:, 512 * h:512 * h + 512],
+                                        True, True), "sq%d" % j))
 
     def cpy(j, q):
-        wait(q, tsq[j])
-        out, in_ = T.SQ[:, PAD + 512 * j:PAD + 512 * j + 512], T["QB%d" % (j % 5)][:]
+        wait(q, tsq[j][1])
+        out, in_ = T.SQ[:, PAD + 512 * j:PAD + 512 * j + 512], T["QB%d" % tsq[j][0]][:]
         tcp[j] = fire(C.activation(out, in_, AF.Copy) if q is qc else V.tensor_copy(out, in_), "cp%d" % j)
 
-    for j in range(4):
+    for j, q in ((0, qc), (2, qv), (1, qc), (3, qv)):
         seq(j)
-        cpy(j, qc if j % 2 == 0 else qv)
-    tg2 = fire(C.activation(T.GB[:, 512:1024], T.PW[:].indirect(T.OW[:, 32:64]), AF.Copy), "gp2")
+        cpy(j, q)
     seq(4)
 
     tlg, tlc, tsy, tii = {}, {}, {}, {}
@@ -261,25 +294,25 @@ def rank_program(g, core, T, topo):
         tvv = fire(V.tensor_tensor(T.VV[:, c], T.XX[:, c], T.MM[:, c], A.mult), "vv")
         wait(qv, tnb, tii[s])
         ti2 = fire(V.tensor_tensor(T.I2[:, c], T.II[:, c], T.NB[:, c], A.add), "i2")
+        wait(qv, ti2, tpf)
+        tot = fire(V.tensor_scalar(T.OT[:, c], T.I2[:, c], PR[:, s:s + 1], None, A.add), "ot")
         if s < 3:
             wait(qv, tvv)
             thi = fire(V.tensor_scalar(T.HI[:, n], T.VV[:, c], 1.0 / 2048, -1023.5 / 2048, A.mult, A.add), "hi")
-        wait(qv, ti2, tpf)
-        tot = fire(V.tensor_scalar(T.OT[:, c], T.I2[:, c], PR[:, s:s + 1], None, A.add), "ot")
         wait(qv, tot, tpad, *[tcp[j] for j in range(4 * s + 4)])
         tgb = fire(V.tensor_tensor(MB[:], T.SQ[:, 0:PAD + 2048 * (s + 1)].indirect(T.OT[:, c]), T.MK[:], A.mult), "gb")
         if s < 3:
             wait(qv, thi)
             tnh = fire(V.tensor_scalar(T.NH[:, c], T.HI[:, n], -2048, None, A.mult), "nh")
-            thh = fire(V.tensor_scalar(T.HH[:, n], T.HI[:, n], 2048, None, A.add), "hh")
-        wait(qv, tgb)
-        tsb = fire(V.tensor_tensor_scan(SB[:], T.K16[:], MB[:], 0.0, A.mult, A.add), "sb")
+        wait(qv, tgb, tkbb)
+        tsb = fire(V.tensor_tensor_scan(SB[:], T.KB[:], MB[:], 0.0, A.mult, A.add), "sb")
         b = SB[:, 15:256:16]
         if s < 3:
             wait(qv, tnh)
             tdd = fire(V.tensor_tensor(T.DD[:, c], T.VV[:, c], T.NH[:, c], A.add), "dd")
             wait(qv, tsb, tdd)
             tsl = fire(V.tensor_tensor(T.SL[:, n], b, T.DD[:, c], A.add), "sl")
+            thh = fire(V.tensor_scalar(T.HH[:, n], T.HI[:, n], 2048, None, A.add), "hh")
             wait(qv, tsl)
             toff[s + 1] = fire(V.tensor_copy(T.OF[:, n], T.SL[:, n]), "of")
         else:
@@ -287,7 +320,6 @@ def rank_program(g, core, T, topo):
             tfn = fire(V.tensor_tensor(T.FN[:], b, T.VV[:, c], A.add), "fn")
     compact(3)
 
-    m0 = slice(16 * me, 16 * me + 16)
     half = {0: slice(0, 64), 1: slice(64, 128), 2: slice(0, 128), 3: slice(0, 64)}
 
     def put(s, out, own, so, sw):

@@ -15,7 +15,7 @@ SCRATCH = {
     "MW": ("sbuf", [128, 2048], "int32"), "PW": ("sbuf", [128, 512], "int32"),
     "LW": ("sbuf", [128, 2048], "bfloat16"), "SQ": ("sbuf", [128, PAD + 8192], "bfloat16"),
     "BI": ("sbuf", [128, 128], "int32"), "BJ": ("sbuf", [128, 128], "int32"), "BF": ("sbuf", [128, 128], "float32"),
-    "OW": ("sbuf", [128, 64], "uint16"), "P8": ("sbuf", [128, 1024], "int32"), "P9": ("sbuf", [128, 1024], "int32"),
+    "OW": ("sbuf", [128, 64], "uint16"), "P8": ("sbuf", [128, 1024], "int32"),
     "PB": ("sbuf", [128, 1024], "bfloat16"), "ZM": ("sbuf", [128, 1024], "bfloat16"), "GB": ("sbuf", [128, 1024], "bfloat16"),
     "IT": ("sbuf", [128, 272], "int32"), "IA": ("sbuf", [128, 272], "int32"), "QI": ("sbuf", [128, 8], "int32"),
     "KI": ("sbuf", [128, 8], "int32"), "GI": ("sbuf", [128, 128], "int32"), "GS": ("sbuf", [128, 128], "bfloat16"),
@@ -27,32 +27,32 @@ SCRATCH = {
     "X0": ("sbuf", [128, 16], "int32"), "L0": ("sbuf", [128, 16], "int32"),
     "OF": ("sbuf", [128, 64], "uint16"), "OT": ("sbuf", [128, 64], "uint16"),
     "HI": ("sbuf", [128, 64], "int32"), "HH": ("sbuf", [128, 64], "float32"), "SL": ("sbuf", [128, 64], "float32"),
-    "AA": ("sbuf", [128, 64], "float32"), "A4": ("sbuf", [128, 64], "float32"), "FF": ("sbuf", [128, 64], "int32"),
+    "AA": ("sbuf", [128, 64], "float32"), "FF": ("sbuf", [128, 64], "int32"),
     "Q4": ("sbuf", [128, 64], "float32"), "QQ": ("sbuf", [128, 64], "float32"), "PP": ("sbuf", [128, 64], "float32"),
     "RR": ("sbuf", [128, 64], "bfloat16"), "II": ("sbuf", [128, 64], "bfloat16"), "XX": ("sbuf", [128, 64], "float32"),
     "MM": ("sbuf", [128, 64], "float32"), "NB": ("sbuf", [128, 64], "float32"), "VV": ("sbuf", [128, 64], "float32"),
-    "NH": ("sbuf", [128, 64], "float32"), "DD": ("sbuf", [128, 64], "float32"),
-    "I2": ("sbuf", [128, 64], "float32"), "SY": ("sbuf", [128, 64], "float32"), "FN": ("sbuf", [128, 16], "float32"),
-    "PR0": ("psum", [128, 512], "float32"), "PR1": ("psum", [128, 512], "float32"), "CP": ("psum", [128, 512], "float32"),
+    "NH": ("sbuf", [128, 64], "float32"), "DD": ("sbuf", [128, 64], "float32"), "I2": ("sbuf", [128, 64], "float32"),
+    "LG": ("sbuf", [128, 1024], "bfloat16"), "SY": ("sbuf", [128, 64], "float32"), "FN": ("sbuf", [128, 16], "float32"),
+    "PR0": ("psum", [128, 512], "float32"), "PR1": ("psum", [128, 512], "float32"),
+    "CP": ("psum", [128, 512], "float32"), "CQ": ("psum", [128, 512], "float32"),
 }
 for _s in range(S):
     SCRATCH["MA%d" % _s] = ("sbuf", [128, 256], "float32")
     SCRATCH["SA%d" % _s] = ("sbuf", [128, 256], "float32")
     SCRATCH["MB%d" % _s] = ("sbuf", [128, 256], "bfloat16")
     SCRATCH["SB%d" % _s] = ("sbuf", [128, 256], "bfloat16")
-    SCRATCH["LG%d" % _s] = ("sbuf", [128, 256], "bfloat16")
-for _b in range(5):
+for _b in range(4):
     SCRATCH["QB%d" % _b] = ("psum", [128, 512], "float32")
 
 SEMAPHORES = (["aS", "aA", "aB", "aC", "aY", "aZ", "aF", "sent"]
-              + ["dB", "dC", "wC", "nC", "dS", "dA", "oS", "oA", "oB", "oC", "dPl", "dP8", "dX", "dPW", "dMWa", "dMWb", "dLW"]
+              + ["dB", "dC", "wC", "nC", "dS", "dA", "oS", "oA", "oB", "oC", "dPl", "dP8", "dX", "dPW", "pi", "dMWa", "dMWb", "dLW"]
               + ["dY", "dZ", "dF3", "dFl", "oY", "oZ", "oF3", "oFl", "out1", "out2"]
-              + ["mLW", "it", "qi", "ki", "gi", "gs", "qa", "qd", "qf", "pF", "p9", "pb", "zt", "zm0", "zm1",
+              + ["mLW", "it", "qi", "ki", "gi", "gs", "qa", "qd", "qf", "pF", "pb", "za", "zt", "zm0", "zm1",
                  "ia", "mk", "k16", "k16b", "kb", "kbb", "on", "su", "es", "id", "cs", "sk", "pad",
                  "bj", "bf", "tp", "ow", "gp0", "gp1"]
               + ["sq%d" % j for j in range(16)] + ["cp%d" % j for j in range(16)]
-              + ["lo", "hi", "hh", "of", "sl", "ga", "aa", "a4", "sa", "ff", "q4", "pp", "qq", "rr", "ii", "pf", "xx", "m2", "nb",
-                 "vv", "nh", "i2", "ot", "gb", "dd", "sb", "fn", "lg", "lc", "sy"])
+              + ["lo", "hi", "hh", "of", "sl", "ga", "aa", "sa", "ff", "q4", "pp", "qq", "rr", "ii", "pf", "xx", "m2", "nb",
+                 "vv", "nh", "i2", "ot", "gb", "dd", "sb", "fn", "lg", "lc0", "lc3", "sy"])
 
 
 def rank_program(g, core, T, topo):
@@ -99,24 +99,27 @@ def rank_program(g, core, T, topo):
         return (sem, len(tr))
 
     m0 = slice(16 * me, 16 * me + 16)
-    tdA = fire(Y.dma_start(T.pA[:], T.models[:]), "dA", 16)
     tdB = fire(C.dma_start(T.pB[:], T.stock[:]), "dB", 16)
+    tdA = fire(Y.dma_start(T.pA[:], T.models[:]), "dA", 16)
     tdS = fire(Y.dma_start(T.pS[:], T.states[:]), "dS", 16)
     twC = fire(C.dma_start(T.CW[:], T.letters[:]), "wC", 16)
-    tP8 = fire(Y.dma_start(T.P8[0:8, :], T.places[me]), "dP8", 16)
+    for h in range(2):
+        tP8 = fire(Y.dma_start(T.P8[0:8, 512 * h:512 * h + 512], T.places[me, 4096 * h:4096 * h + 4096]), "dP8", 16)
     toA = fire(C.dma_start(T.lA[me], T.models[me]), "oA", 16)
     toS = fire(Y.dma_start(T.lS[me], T.states[me]), "oS", 16)
     toB = fire(C.dma_start(T.lB[me], T.stock[me]), "oB", 16)
-    for k in range(8):
-        tPl = fire((Y if k % 2 else C).dma_start(T.BI[0:64, 16 * k:16 * k + 16], T.places[me, 1024 * k:1024 * k + 1024]), "dPl", 16)
+    for h in range(2):
+        for k in range(8):
+            t = 4096 * h + 512 * k
+            tPl = fire((Y if k % 2 else C).dma_start(T.BI[32 * h:32 * h + 32, 16 * k:16 * k + 16], T.places[me, t:t + 512]), "dPl", 16)
     tit = fire(g.iota(T.IT[:], [[1, 272]], -15, -1), "it")
     tgi = fire(g.iota(T.GI[0:8, :], [[1, 8], [0, 16]], 0, -1), "gi")
     tqi = fire(g.iota(T.QI[:], [[0, 8]], 0, 1), "qi")
     tki = fire(g.iota(T.KI[:], [[1, 8]], 0, 0), "ki")
-    wait(qg, tdA)
-    aA = send("pA", "lA", "aA")
     wait(qg, tdB)
     aB = send("pB", "lB", "aB")
+    wait(qg, tdA)
+    aA = send("pA", "lA", "aA")
     wait(qg, tdS)
     aS = send("pS", "lS", "aS")
 
@@ -137,52 +140,52 @@ def rank_program(g, core, T, topo):
     tqa = fire(V.tensor_scalar(T.QA[:], T.QI[:], 15, None, A.bitwise_and), "qa")
     tqd = fire(V.tensor_scalar(T.QD[:], T.QI[:], 4, None, A.arith_shift_right), "qd")
     wait(qv, tqa)
-    tqf = fire(V.tensor_copy(T.QF[:], T.QA[:]), "qf")
+    tqf = fire(V.tensor_scalar(T.QF[:], T.QA[:], 144, None, A.add), "qf")
     wait(qv, tqd)
     tpF = fire(V.tensor_copy(T.PF[:], T.QD[:]), "pF")
     wait(qv, tpF)
     tcs = fire(V.tensor_scalar(T.CS[:], T.KI[:], T.PF[:, 0:1], None, A.is_equal), "cs")
-    wait(qv, tP8)
-    tp9 = fire(V.tensor_scalar(T.P9[0:8, :], T.P8[0:8, :], 9, None, A.arith_shift_right), "p9")
-    wait(qv, twC)
-    tnC = fire(V.tensor_copy(T.CN[:], T.CW[:]), "nC")
-    wait(qv, tp9)
-    tpb = fire(V.tensor_copy(T.PB[0:8, :], T.P9[0:8, :]), "pb")
-    wait(qv, tPl)
-    tbj = fire(V.tensor_scalar(T.BJ[0:64, :], T.BI[0:64, :], 511, None, A.bitwise_and), "bj")
     wait(qv, tmk)
     tes = fire(V.tensor_scalar(T.ES[:], T.IT[:, 0:144], 0, T.MK[:, 0:1], A.is_equal, A.mult), "es")
+    tpad = fire(V.memset(T.SQ[:, 0:PAD], 0.0), "pad")
+    wait(qv, tP8)
+    tpb = fire(V.tensor_scalar(T.PB[0:8, :], T.P8[0:8, :], 1.0 / 512, 143.501, A.mult, A.add), "pb")
+    wait(qv, tPl)
+    tbj = fire(V.tensor_scalar(T.BJ[0:64, :], T.BI[0:64, :], 511, None, A.bitwise_and), "bj")
+    wait(qv, twC)
+    tnC = fire(V.tensor_copy(T.CN[:], T.CW[:]), "nC")
     wait(qv, tbj)
     tbf = fire(V.tensor_copy(T.BF[0:64, :], T.BJ[0:64, :]), "bf")
-    tpad = fire(V.memset(T.SQ[:, 0:PAD], 0.0), "pad")
+    tmLW = fire(V.memset(T.LW[:], 0.0), "mLW")
     wait(qt, tgs, tpb)
-    TE.matmul(T.QB0[:], T.GS[0:8, :], T.PB[0:8, 0:512], True, True)
+    tza = fire(TE.matmul(T.QB0[:], T.GS[0:8, :], T.PB[0:8, 0:512], True, True), "za")
     tzt = fire(TE.matmul(T.QB1[:], T.GS[0:8, :], T.PB[0:8, 512:1024], True, True), "zt")
     wait(qt, tid, tbf)
     ttp = fire(TE.transpose(T.CP[:, 64:128], T.BF[0:64, :], T.ID[0:64, 0:64]), "tp")
-    wait(qv, tzt, tqf)
+    wait(qv, tza, tqf)
     tz0 = fire(V.tensor_scalar(T.ZM[:, 0:512], T.QB0[:], T.QF[:, 0:1], None, A.is_equal), "zm0")
-    tz1 = fire(V.tensor_scalar(T.ZM[:, 512:1024], T.QB1[:], T.QF[:, 0:1], None, A.is_equal), "zm1")
     wait(qv, ttp)
     tow = fire(V.tensor_copy(T.OW[:], T.CP[:, 64:128]), "ow")
-    tmLW = fire(V.memset(T.LW[:], 0.0), "mLW")
+    wait(qv, tzt)
+    tz1 = fire(V.tensor_scalar(T.ZM[:, 512:1024], T.QB1[:], T.QF[:, 0:1], None, A.is_equal), "zm1")
 
     wait(qc, tnC)
     tdC = fire(C.dma_start(T.pC[:], T.CN[:]), "dC", 16)
     toC = fire(C.dma_start(T.lC[me], T.CN[m0, :]), "oC", 16)
     wait(qg, tdC)
     aC = send("pC", "lC", "aC")
-    wait(qc, aA, toA)
-    for q in range(8, 16):
-        tMb = fire(C.dma_start(T.MW[q:128:16, :], T.lA[:]), "dMWb", 16)
     wait(qy, aB, toB)
     for k in range(8):
         tPW = fire(Y.dma_start(T.PW[16 * k:16 * k + 16, :], T.lB[:]), "dPW", 16)
-    wait(qy, aA, toA)
-    for q in range(8):
-        tMa = fire(Y.dma_start(T.MW[q:128:16, :], T.lA[:]), "dMWa", 16)
-    wait(qy, aS, toS)
+    Y.sem_inc(T.sem.pi, 1)
+    count["pi"] = 1
+    wait(qc, aA, toA, ("pi", 1))
+    for q in range(10):
+        tMb = fire(C.dma_start(T.MW[q:128:16, :], T.lA[:]), "dMWb", 16)
+    wait(qy, aA, aS, toA, toS)
     tX = fire(Y.dma_start(T.X0[:], T.lS[:]), "dX", 16)
+    for q in range(10, 16):
+        tMa = fire(Y.dma_start(T.MW[q:128:16, :], T.lA[:]), "dMWa", 16)
     wait(qy, aC, toC, tmLW)
     tLW = fire(Y.dma_start(T.LW[0:128:16, :], T.lC[:]), "dLW", 16)
     wait(qc, ton, tcs)
@@ -190,8 +193,12 @@ def rank_program(g, core, T, topo):
         tsk = fire(C.activation(T.SK[:, 128 * k:128 * k + 128], T.ON[:], AF.Copy, scale=T.CS[:, k:k + 1]), "sk")
 
     wait(qv, tow, tz0, tz1, tPW)
-    tg0 = fire(V.tensor_tensor(T.GB[:, 0:512], T.PW[:].indirect(T.OW[:, 0:32]), T.ZM[:, 0:512], A.mult), "gp0")
-    tg1 = fire(V.tensor_tensor(T.GB[:, 512:1024], T.PW[:].indirect(T.OW[:, 32:64]), T.ZM[:, 512:1024], A.mult), "gp1")
+
+    def pick(h):
+        return fire(V.tensor_tensor(T.GB[:, 512 * h:512 * h + 512], T.PW[:].indirect(T.OW[:, 32 * h:32 * h + 32]),
+                                    T.ZM[:, 512 * h:512 * h + 512], A.mult), "gp%d" % h)
+
+    tg = {0: pick(0)}
     wait(qv, tX)
     tlo = fire(V.tensor_scalar(T.L0[:], T.X0[:], 2047, None, A.bitwise_and), "lo")
     thi = fire(V.tensor_scalar(T.HI[:, 0:16], T.X0[:], 11, None, A.arith_shift_right), "hi")
@@ -200,44 +207,44 @@ def rank_program(g, core, T, topo):
     tsl = fire(V.tensor_copy(T.SL[:, 0:16], T.L0[:]), "sl")
     wait(qv, thi)
     thh = fire(V.tensor_scalar(T.HH[:, 0:16], T.HI[:, 0:16], 2048, None, A.add), "hh")
-
     tcp, tsq, banks = {}, {}, []
 
     def seq(j):
-        wait(qt, tsk, tz0, tz1, tg1 if j % 2 else tg0)
+        wait(qt, tsk, tz0, tz1, tg[j // 8])
         n = len(banks)
-        if n >= 5:
-            wait(qt, tcp[banks[n - 5]])
+        if n >= 4:
+            wait(qt, tcp[banks[n - 4]])
         banks.append(j)
-        k, h = j // 2, j % 2
-        tsq[j] = (n % 5, fire(TE.matmul(T["QB%d" % (n % 5)][:], T.SK[:, 128 * k:128 * k + 128], T.GB[:, 512 * h:512 * h + 512],
-                                        True, True), "sq%d" % j))
+        h, k = j // 8, j % 8
+        m = TE.matmul(T["QB%d" % (n % 4)][:], T.SK[:, 128 * k:128 * k + 128], T.GB[:, 512 * h:512 * h + 512], True, True)
+        tsq[j] = (n % 4, fire(m, "sq%d" % j))
 
-    def cpy(j, q):
-        wait(q, tsq[j][1])
-        out, in_ = T.SQ[:, PAD + 512 * j:PAD + 512 * j + 512], T["QB%d" % tsq[j][0]][:]
-        tcp[j] = fire(C.activation(out, in_, AF.Copy) if q is qc else V.tensor_copy(out, in_), "cp%d" % j)
+    def cpy(j):
+        wait(qc, tsq[j][1])
+        tcp[j] = fire(C.activation(T.SQ[:, PAD + 512 * j:PAD + 512 * j + 512], T["QB%d" % tsq[j][0]][:], AF.Copy), "cp%d" % j)
 
-    for j, q in ((0, qc), (2, qv), (1, qc), (3, qv)):
+    for j in range(6):
         seq(j)
-        cpy(j, q)
-    seq(4)
+        cpy(j)
+    tg[1] = pick(1)
 
     tlg, tlc, tsy, tii = {}, {}, {}, {}
 
     def letters(s, tok):
         wait(qc, tok, tLW)
-        tlg[s] = fire(C.activation(T["LG%d" % s][:], T.LW[:].indirect(T.OF[:, 16 * s:16 * s + 16]), AF.Copy), "lg")
+        tlg[s] = fire(C.activation(T.LG[:, 256 * s:256 * s + 256], T.LW[:].indirect(T.OF[:, 16 * s:16 * s + 16]), AF.Copy), "lg")
 
-    def compact(s):
-        wait(qt, tlg[s], tes, tow)
-        if s:
-            wait(qt, tsy[s - 1])
-        for q in range(16):
-            m = TE.matmul(T.CP[:, 16 * s:16 * s + 16], T.ES[:, 15 - q:143 - q], T["LG%d" % s][:, q:256:16], q == 0, q == 15)
-        tlc[s] = fire(m, "lc")
-        wait(qc, tlc[s])
-        tsy[s] = fire(C.activation(T.SY[:, 16 * s:16 * s + 16], T.CP[:, 16 * s:16 * s + 16], AF.Copy), "sy")
+    def compact(a, b, lo=0, hi=16):
+        wait(qt, tlg[b - 1], tes, tow)
+        CP = T.CQ if a else T.CP
+        for q in range(lo, hi):
+            m = TE.matmul(CP[:, 0:16 * (b - a)], T.ES[:, 15 - q:143 - q], T.LG[:, 256 * a + q:256 * b:16], q == 0, q == 15)
+        if hi == 16:
+            tlc[a] = fire(m, "lc%d" % a)
+
+    def collect(a, b):
+        wait(qc, tlc[a])
+        tsy[a] = fire(C.activation(T.SY[:, 16 * a:16 * b], (T.CQ if a else T.CP)[:, 0:16 * (b - a)], AF.Copy), "sy")
 
     toff = {0: tof}
     for s in range(S):
@@ -252,20 +259,20 @@ def rank_program(g, core, T, topo):
         taa = fire(V.tensor_tensor(T.AA[:, c], T.HI[:, c], T.SL[:, c], A.add), "aa")
         wait(qv, tga, tk6b)
         tsa = fire(V.tensor_tensor_scan(SA[:], T.K16[:], MA[:], 0.0, A.mult, A.add), "sa")
-        wait(qv, taa)
-        ta4 = fire(V.tensor_scalar(T.A4[:, c], T.AA[:, c], -4096, None, A.add), "a4")
+        if s:
+            thh = fire(V.tensor_scalar(T.HH[:, c], T.HI[:, c], 2048, None, A.add), "hh")
         wait(qv, tsa)
         e = SA[:, 15:256:16]
         tff = fire(V.tensor_scalar(T.FF[:, c], e, 1.0 / 2048, -1023.5 / 2048, A.mult, A.add), "ff")
-        wait(qv, ta4)
-        tq4 = fire(V.tensor_tensor(T.Q4[:, c], e, T.A4[:, c], A.subtract), "q4")
+        wait(qv, taa)
+        tqq = fire(V.tensor_tensor(T.QQ[:, c], e, T.AA[:, c], A.subtract), "qq")
         wait(qv, tff, thh)
         tpp = fire(V.tensor_tensor(T.PP[:, c], T.FF[:, c], T.HH[:, c], A.mult), "pp")
-        tqq = fire(V.tensor_tensor(T.QQ[:, c], T.AA[:, c], e, A.subtract), "qq")
+        wait(qv, tqq)
+        tq4 = fire(V.tensor_scalar(T.Q4[:, c], T.QQ[:, c], 4096, None, A.add), "q4")
         wait(qv, tpp, tq4)
         trr = fire(V.tensor_tensor(T.RR[:, c], T.PP[:, c], T.Q4[:, c], A.is_lt), "rr")
-        wait(qv, tqq)
-        txx = fire(V.tensor_tensor(T.XX[:, c], T.PP[:, c], T.QQ[:, c], A.add), "xx")
+        txx = fire(V.tensor_tensor(T.XX[:, c], T.PP[:, c], T.QQ[:, c], A.subtract), "xx")
         wait(qv, trr, ton)
         tii[s] = fire(V.tensor_tensor_scan(T.II[:, c], T.ON[:, 0:16], T.RR[:, c], 0.0, A.mult, A.add), "ii")
         tm2 = fire(V.tensor_scalar(T.MM[:, c], T.RR[:, c], 255, 1, A.mult, A.add), "m2")
@@ -276,54 +283,57 @@ def rank_program(g, core, T, topo):
             wait(qt, tii[s - 1])
         for b in range(s):
             TE.matmul(PR[:, s:s + 1], T.ON[:], T.II[:, 16 * b + 15:16 * b + 16], b == 0, False)
+        if s == 3:
+            letters(3, toff[3])
+            compact(3, 4, 0, 4)
         wait(qt, tii[s])
         tpf = fire(TE.matmul(PR[:, s:s + 1], T.SU[:], T.II[:, 16 * s + 15:16 * s + 16], s == 0, True), "pf")
+        if s in (1, 2):
+            letters(s, toff[s])
+        for j in range(*((6, 11), (11, 14), (14, 16), (0, 0))[s]):
+            seq(j)
+            cpy(j)
         if s == 0:
-            for j in range(4, 8):
-                if j > 4:
-                    seq(j)
-                cpy(j, qc)
-        else:
-            compact(s - 1)
-            if s < 3:
-                for j in range(4 * s + 4, 4 * s + 8):
-                    seq(j)
-                    cpy(j, qc)
-        letters(s, toff[s])
+            letters(0, toff[0])
+        if s == 2:
+            compact(0, 3)
+            collect(0, 3)
+        if s == 3:
+            compact(3, 4, 4, 16)
+            collect(3, 4)
         wait(qv, tm2, txx)
         tvv = fire(V.tensor_tensor(T.VV[:, c], T.XX[:, c], T.MM[:, c], A.mult), "vv")
         wait(qv, tnb, tii[s])
         ti2 = fire(V.tensor_tensor(T.I2[:, c], T.II[:, c], T.NB[:, c], A.add), "i2")
-        wait(qv, ti2, tpf)
-        tot = fire(V.tensor_scalar(T.OT[:, c], T.I2[:, c], PR[:, s:s + 1], None, A.add), "ot")
         if s < 3:
             wait(qv, tvv)
             thi = fire(V.tensor_scalar(T.HI[:, n], T.VV[:, c], 1.0 / 2048, -1023.5 / 2048, A.mult, A.add), "hi")
-        wait(qv, tot, tpad, *[tcp[j] for j in range(4 * s + 4)])
-        tgb = fire(V.tensor_tensor(MB[:], T.SQ[:, 0:PAD + 2048 * (s + 1)].indirect(T.OT[:, c]), T.MK[:], A.mult), "gb")
+        wait(qv, ti2, tpf)
+        tot = fire(V.tensor_scalar(T.OT[:, c], T.I2[:, c], PR[:, s:s + 1], None, A.add), "ot")
         if s < 3:
             wait(qv, thi)
             tnh = fire(V.tensor_scalar(T.NH[:, c], T.HI[:, n], -2048, None, A.mult), "nh")
+        wait(qv, tot, tpad, *[tcp[j] for j in range(4 * s + 4)])
+        tgb = fire(V.tensor_tensor(MB[:], T.SQ[:, 0:PAD + 2048 * (s + 1)].indirect(T.OT[:, c]), T.MK[:], A.mult), "gb")
+        if s < 3:
+            wait(qv, tnh)
+            tdd = fire(V.tensor_tensor(T.DD[:, c], T.VV[:, c], T.NH[:, c], A.add), "dd")
         wait(qv, tgb, tkbb)
         tsb = fire(V.tensor_tensor_scan(SB[:], T.KB[:], MB[:], 0.0, A.mult, A.add), "sb")
         b = SB[:, 15:256:16]
         if s < 3:
-            wait(qv, tnh)
-            tdd = fire(V.tensor_tensor(T.DD[:, c], T.VV[:, c], T.NH[:, c], A.add), "dd")
             wait(qv, tsb, tdd)
             tsl = fire(V.tensor_tensor(T.SL[:, n], b, T.DD[:, c], A.add), "sl")
-            thh = fire(V.tensor_scalar(T.HH[:, n], T.HI[:, n], 2048, None, A.add), "hh")
             wait(qv, tsl)
             toff[s + 1] = fire(V.tensor_copy(T.OF[:, n], T.SL[:, n]), "of")
         else:
             wait(qv, tsb, tvv)
             tfn = fire(V.tensor_tensor(T.FN[:], b, T.VV[:, c], A.add), "fn")
-    compact(3)
 
     half = {0: slice(0, 64), 1: slice(64, 128), 2: slice(0, 128), 3: slice(0, 64)}
 
     def put(s, out, own, so, sw):
-        wait(qy, tsy[s])
+        wait(qy, tsy[3 if s == 3 else 0])
         c = slice(16 * s, 16 * s + 16)
         a = fire(Y.dma_start(out[:, half[s], :], T.SY[:, c]), so, 16)
         b = fire(Y.dma_start(own[me, half[s], :], T.SY[m0, c]), sw, 16)
@@ -337,9 +347,8 @@ def rank_program(g, core, T, topo):
     wait(qg, a)
     aZ = send("rZ", "lZ", "aZ")
     a, oF3 = put(3, T.rF, T.lF, "dF3", "oF3")
-    wait(qy, tfn)
-    b = fire(Y.dma_start(T.rF[:, 64:128, :], T.FN[:]), "dFl", 16)
     wait(qc, tfn)
+    b = fire(C.dma_start(T.rF[:, 64:128, :], T.FN[:]), "dFl", 16)
     oFl = fire(C.dma_start(T.lF[me, 64:128, :], T.FN[m0, :]), "oFl", 16)
     wait(qg, a, b)
     aF = send("rF", "lF", "aF")

@@ -2,7 +2,12 @@ import numpy as np
 from concourse.bass import DstId, RemoteDMATransfer
 from concourse.mybir import dt, AluOpType, AxisListType, ActivationFunctionType
 
-N, S, PAD, BIG = 8, 4, 16, 20000
+N, S, PAD, BIG = 8, 4, 16, 16384
+E22 = 4194304
+CV = (8, 6, 6, 6)
+CW = (16, 6, 6, 6)
+SLOT_A = ((8,), (6, 7), (0, 1), ())
+SLOT_B = ((), (12,), (2,), ())
 
 SCRATCH = {
     "pS": ("dram", [8, 128, 2], "int32"), "pA": ("dram", [8, 128, 16], "int32"),
@@ -14,24 +19,27 @@ SCRATCH = {
     "CW": ("sbuf", [128, 128], "int32"), "CN": ("sbuf", [128, 128], "bfloat16"),
     "MW": ("sbuf", [128, 2048], "int32"), "PW": ("sbuf", [128, 512], "int32"),
     "LW": ("sbuf", [128, 2048], "bfloat16"), "SQ": ("sbuf", [128, PAD + 8192], "bfloat16"),
+    "R8": ("sbuf", [128, 512], "bfloat16"), "R12": ("sbuf", [128, 512], "bfloat16"),
     "BI": ("sbuf", [128, 128], "int32"), "BJ": ("sbuf", [128, 128], "int32"), "BF": ("sbuf", [128, 128], "float32"),
     "OW": ("sbuf", [128, 64], "uint16"), "P8": ("sbuf", [128, 1024], "int32"),
     "PB": ("sbuf", [128, 1024], "bfloat16"), "ZM": ("sbuf", [128, 1024], "bfloat16"), "GB": ("sbuf", [128, 1024], "bfloat16"),
-    "IT": ("sbuf", [128, 272], "int32"), "IA": ("sbuf", [128, 272], "int32"), "QI": ("sbuf", [128, 8], "int32"),
+    "IT": ("sbuf", [128, 160], "int32"), "IA": ("sbuf", [128, 16], "int32"), "QI": ("sbuf", [128, 8], "int32"),
     "KI": ("sbuf", [128, 8], "int32"), "GI": ("sbuf", [128, 128], "int32"), "GS": ("sbuf", [128, 128], "bfloat16"),
     "QA": ("sbuf", [128, 8], "int32"), "QD": ("sbuf", [128, 8], "int32"), "QF": ("sbuf", [128, 8], "float32"),
-    "PF": ("sbuf", [128, 8], "float32"),
-    "MK": ("sbuf", [128, 256], "float32"), "K16": ("sbuf", [128, 256], "float32"), "KB": ("sbuf", [128, 256], "bfloat16"),
+    "PF": ("sbuf", [128, 8], "float32"), "QL": ("sbuf", [128, 8], "float32"),
+    "EB": ("sbuf", [128, 8], "float32"), "BB": ("sbuf", [128, 8], "float32"), "KE": ("sbuf", [128, 8], "float32"),
+    "M0": ("sbuf", [128, 16], "float32"), "M1": ("sbuf", [128, 16], "float32"), "M2": ("sbuf", [128, 16], "bfloat16"),
+    "ME": ("sbuf", [128, 256], "float32"), "MB": ("sbuf", [128, 256], "bfloat16"),
     "ON": ("sbuf", [128, 128], "bfloat16"), "SU": ("sbuf", [128, 128], "bfloat16"), "ES": ("sbuf", [128, 144], "bfloat16"),
-    "ID": ("sbuf", [128, 128], "float32"), "CS": ("sbuf", [128, 8], "float32"), "SK": ("sbuf", [128, 1024], "bfloat16"),
-    "X0": ("sbuf", [128, 16], "int32"), "L0": ("sbuf", [128, 16], "int32"),
+    "ID": ("sbuf", [128, 128], "float32"), "IB": ("sbuf", [128, 128], "bfloat16"), "IG": ("sbuf", [128, 128], "bfloat16"),
+    "CS": ("sbuf", [128, 8], "float32"), "SK": ("sbuf", [128, 1024], "bfloat16"),
+    "X0": ("sbuf", [128, 16], "int32"), "L0": ("sbuf", [128, 16], "int32"), "H0": ("sbuf", [128, 16], "int32"),
     "OF": ("sbuf", [128, 64], "uint16"), "OT": ("sbuf", [128, 64], "uint16"),
-    "HI": ("sbuf", [128, 64], "int32"), "HH": ("sbuf", [128, 64], "float32"), "SL": ("sbuf", [128, 64], "float32"),
+    "HH": ("sbuf", [128, 64], "int32"), "SL": ("sbuf", [128, 64], "float32"),
     "AA": ("sbuf", [128, 64], "float32"), "FF": ("sbuf", [128, 64], "int32"),
     "Q4": ("sbuf", [128, 64], "float32"), "QQ": ("sbuf", [128, 64], "float32"), "PP": ("sbuf", [128, 64], "float32"),
-    "RR": ("sbuf", [128, 64], "bfloat16"), "II": ("sbuf", [128, 64], "bfloat16"), "XX": ("sbuf", [128, 64], "float32"),
-    "MM": ("sbuf", [128, 64], "float32"), "NB": ("sbuf", [128, 64], "float32"), "VV": ("sbuf", [128, 64], "float32"),
-    "NH": ("sbuf", [128, 64], "float32"), "DD": ("sbuf", [128, 64], "float32"), "I2": ("sbuf", [128, 64], "float32"),
+    "RR": ("sbuf", [128, 128], "bfloat16"), "II": ("sbuf", [128, 128], "bfloat16"), "XX": ("sbuf", [128, 64], "float32"),
+    "MM": ("sbuf", [128, 64], "float32"), "VV": ("sbuf", [128, 64], "int32"), "DD": ("sbuf", [128, 64], "int32"),
     "LG": ("sbuf", [128, 1024], "bfloat16"), "SY": ("sbuf", [128, 64], "float32"), "FN": ("sbuf", [128, 16], "float32"),
     "PR0": ("psum", [128, 512], "float32"), "PR1": ("psum", [128, 512], "float32"),
     "CP": ("psum", [128, 512], "float32"), "CQ": ("psum", [128, 512], "float32"),
@@ -39,7 +47,7 @@ SCRATCH = {
 for _s in range(S):
     SCRATCH["MA%d" % _s] = ("sbuf", [128, 256], "float32")
     SCRATCH["SA%d" % _s] = ("sbuf", [128, 256], "float32")
-    SCRATCH["MB%d" % _s] = ("sbuf", [128, 256], "bfloat16")
+    SCRATCH["GM%d" % _s] = ("sbuf", [128, 256], "bfloat16")
     SCRATCH["SB%d" % _s] = ("sbuf", [128, 256], "bfloat16")
 for _b in range(4):
     SCRATCH["QB%d" % _b] = ("psum", [128, 512], "float32")
@@ -47,12 +55,12 @@ for _b in range(4):
 SEMAPHORES = (["aS", "aA", "aB", "aC", "aY", "aZ", "aF", "sent"]
               + ["dB", "dC", "wC", "nC", "dS", "dA", "oS", "oA", "oB", "oC", "dPl", "dP8", "dX", "dPW", "pi", "dMWa", "dMWb", "dLW"]
               + ["dY", "dZ", "dF3", "dFl", "oY", "oZ", "oF3", "oFl", "out1", "out2"]
-              + ["mLW", "it", "qi", "ki", "gi", "gs", "qa", "qd", "qf", "pF", "pb", "za", "zt", "zm0", "zm1",
-                 "ia", "mk", "k16", "k16b", "kb", "kbb", "on", "su", "es", "id", "cs", "sk", "pad",
+              + ["dR8", "dR12", "m2b", "mm", "pb1", "kg", "it", "qi", "ki", "gi", "gs", "qa", "qd", "qf", "pF", "pb", "za", "zt",
+                 "zm0", "zm1", "ia", "ql", "kf", "m0", "m1", "me", "on", "su", "es", "ez", "id", "igb", "cs", "sk", "pad", "rz",
                  "bj", "bf", "tp", "ow", "gp0", "gp1"]
-              + ["sq%d" % j for j in range(16)] + ["cp%d" % j for j in range(16)]
-              + ["lo", "hi", "hh", "of", "sl", "ga", "aa", "sa", "ff", "q4", "pp", "qq", "rr", "ii", "pf", "xx", "m2", "nb",
-                 "vv", "nh", "i2", "ot", "gb", "dd", "sb", "fn", "lg", "lc0", "lc3", "sy"])
+              + ["sq%d" % j for j in range(13)] + ["cp%d" % j for j in range(13)]
+              + ["lo", "hi", "hh", "of", "sl", "ga", "gc", "aa", "sa", "ff", "q4", "pp", "qq", "rr", "ii", "pf", "xx", "m2",
+                 "vv", "ot", "gb", "hb", "dd", "sb", "fn", "lg", "lc0", "lc3", "sy"])
 
 
 def rank_program(g, core, T, topo):
@@ -112,7 +120,7 @@ def rank_program(g, core, T, topo):
         for k in range(8):
             t = 4096 * h + 512 * k
             tPl = fire((Y if k % 2 else C).dma_start(T.BI[32 * h:32 * h + 32, 16 * k:16 * k + 16], T.places[me, t:t + 512]), "dPl", 16)
-    tit = fire(g.iota(T.IT[:], [[1, 272]], -15, -1), "it")
+    tit = fire(g.iota(T.IT[:], [[1, 160]], -15, -1), "it")
     tgi = fire(g.iota(T.GI[0:8, :], [[1, 8], [0, 16]], 0, -1), "gi")
     tqi = fire(g.iota(T.QI[:], [[0, 8]], 0, 1), "qi")
     tki = fire(g.iota(T.KI[:], [[1, 8]], 0, 0), "ki")
@@ -124,44 +132,59 @@ def rank_program(g, core, T, topo):
     aS = send("pS", "lS", "aS")
 
     ton = fire(V.memset(T.ON[:], 1.0), "on")
-    tk6 = fire(V.memset(T.K16[:], 1.0), "k16")
-    tkb = fire(V.memset(T.KB[:], 1.0), "kb")
+    trz = fire(V.memset(T.RR[:], 0.0), "rz")
+    tpad = fire(V.memset(T.SQ[:, 0:PAD], -256.0), "pad")
     wait(qv, tit)
-    tia = fire(V.tensor_scalar(T.IA[:], T.IT[:], 15, None, A.bitwise_and), "ia")
     tid = fire(V.tensor_scalar(T.ID[:], T.IT[:, 15:143], 0, None, A.is_equal), "id")
-    tsu = fire(V.tensor_scalar(T.SU[:], T.IT[:, 15:143], 0, None, A.is_gt), "su")
-    wait(qv, tia)
-    tmk = fire(V.tensor_scalar(T.MK[:], T.IA[:, 15:271], 0, None, A.is_equal), "mk")
-    wait(qv, tk6, tkb)
-    tk6b = fire(V.memset(T.K16[:, 0:256:16], 0.0), "k16b")
-    tkbb = fire(V.memset(T.KB[:, 0:256:16], 0.0), "kbb")
+    tia = fire(V.tensor_scalar(T.IA[:], T.IT[:, 15:31], 15, None, A.bitwise_and), "ia")
     wait(qv, tgi, tqi, tki)
     tgs = fire(V.tensor_scalar(T.GS[0:8, :], T.GI[0:8, :], 0, None, A.is_equal), "gs")
     tqa = fire(V.tensor_scalar(T.QA[:], T.QI[:], 15, None, A.bitwise_and), "qa")
     tqd = fire(V.tensor_scalar(T.QD[:], T.QI[:], 4, None, A.arith_shift_right), "qd")
-    wait(qv, tqa)
-    tqf = fire(V.tensor_scalar(T.QF[:], T.QA[:], 144, None, A.add), "qf")
-    wait(qv, tqd)
+    wait(qv, tia)
+    tm0 = fire(V.tensor_scalar(T.M0[:], T.IA[:], 0, -2, A.is_equal, A.mult), "m0")
+    tm1 = fire(V.tensor_scalar(T.M1[:], T.IA[:], 1, None, A.is_equal), "m1")
+    wait(qv, tqa, tqd)
+    tql = fire(V.tensor_scalar(T.QL[:], T.QA[:], 15, None, A.is_equal), "ql")
     tpF = fire(V.tensor_copy(T.PF[:], T.QD[:]), "pF")
+    wait(qv, tm0, tm1)
+    tm2 = fire(V.tensor_tensor(T.M2[:], T.M0[:], T.M1[:], A.add), "m2b")
+    tqf = fire(V.tensor_scalar(T.QF[:], T.QA[:], 144, None, A.add), "qf")
     wait(qv, tpF)
     tcs = fire(V.tensor_scalar(T.CS[:], T.KI[:], T.PF[:, 0:1], None, A.is_equal), "cs")
-    wait(qv, tmk)
-    tes = fire(V.tensor_scalar(T.ES[:], T.IT[:, 0:144], 0, T.MK[:, 0:1], A.is_equal, A.mult), "es")
-    tpad = fire(V.memset(T.SQ[:, 0:PAD], 0.0), "pad")
+    tke = fire(V.tensor_scalar(T.KE[:], T.QA[:], 0, None, A.is_equal), "kf")
+    tsu = fire(V.tensor_scalar(T.SU[:], T.IT[:, 15:143], 0, None, A.is_gt), "su")
+    tez = fire(V.memset(T.ES[:], 0.0), "ez")
+    wait(qc, tid)
+    tib = fire(C.activation(T.IB[:], T.ID[:], AF.Copy), "igb")
+    wait(qc, tql)
+    fire(C.activation(T.EB[:], T.QL[:], AF.Copy, scale=float(E22), bias=float(6144 - E22)), "kg")
+    tkg = fire(C.activation(T.BB[:], T.QL[:], AF.Copy, scale=256.0), "kg")
+    wait(qc, ton, tcs)
+    for k in range(8):
+        tsk = fire(C.activation(T.SK[:, 128 * k:128 * k + 128], T.ON[:], AF.Copy, scale=T.CS[:, k:k + 1]), "sk")
+    tig = fire(C.activation(T.IG[:], T.ID[:], AF.Copy, scale=float(BIG)), "igb")
+    wait(qc, tke, tez)
+    tes = fire(C.activation(T.ES[:, 15:143], T.ID[:], AF.Copy, scale=T.KE[:, 0:1]), "es")
+    wait(qt, tib, tm2)
+    for q in range(16):
+        m = TE.matmul(T.PR1[:, 16 * q:16 * q + 16], T.IB[:], T.M2[:], True, True)
+    tmm = fire(m, "mm")
     wait(qv, tP8)
-    tpb = fire(V.tensor_scalar(T.PB[0:8, :], T.P8[0:8, :], 1.0 / 512, 143.501, A.mult, A.add), "pb")
+    tpb = fire(V.tensor_scalar(T.PB[0:8, 0:512], T.P8[0:8, 0:512], 1.0 / 512, 143.501, A.mult, A.add), "pb")
     wait(qv, tPl)
     tbj = fire(V.tensor_scalar(T.BJ[0:64, :], T.BI[0:64, :], 511, None, A.bitwise_and), "bj")
     wait(qv, twC)
     tnC = fire(V.tensor_copy(T.CN[:], T.CW[:]), "nC")
     wait(qv, tbj)
     tbf = fire(V.tensor_copy(T.BF[0:64, :], T.BJ[0:64, :]), "bf")
-    tmLW = fire(V.memset(T.LW[:], 0.0), "mLW")
+    tpc = fire(V.tensor_scalar(T.PB[0:8, 512:1024], T.P8[0:8, 512:1024], 1.0 / 512, 143.501, A.mult, A.add), "pb1")
     wait(qt, tgs, tpb)
     tza = fire(TE.matmul(T.QB0[:], T.GS[0:8, :], T.PB[0:8, 0:512], True, True), "za")
-    tzt = fire(TE.matmul(T.QB1[:], T.GS[0:8, :], T.PB[0:8, 512:1024], True, True), "zt")
     wait(qt, tid, tbf)
     ttp = fire(TE.transpose(T.CP[:, 64:128], T.BF[0:64, :], T.ID[0:64, 0:64]), "tp")
+    wait(qt, tpc)
+    tzt = fire(TE.matmul(T.QB1[:], T.GS[0:8, :], T.PB[0:8, 512:1024], True, True), "zt")
     wait(qv, tza, tqf)
     tz0 = fire(V.tensor_scalar(T.ZM[:, 0:512], T.QB0[:], T.QF[:, 0:1], None, A.is_equal), "zm0")
     wait(qv, ttp)
@@ -169,6 +192,9 @@ def rank_program(g, core, T, topo):
     wait(qv, tzt)
     tz1 = fire(V.tensor_scalar(T.ZM[:, 512:1024], T.QB1[:], T.QF[:, 0:1], None, A.is_equal), "zm1")
 
+    wait(qc, tmm)
+    tme = fire(C.activation(T.ME[:], T.PR1[:, 0:256], AF.Copy, scale=float(E22)), "me")
+    tmb = fire(C.activation(T.MB[:], T.PR1[:, 0:256], AF.Copy, scale=256.0), "igb")
     wait(qc, tnC)
     tdC = fire(C.dma_start(T.pC[:], T.CN[:]), "dC", 16)
     toC = fire(C.dma_start(T.lC[me], T.CN[m0, :]), "oC", 16)
@@ -186,56 +212,68 @@ def rank_program(g, core, T, topo):
     tX = fire(Y.dma_start(T.X0[:], T.lS[:]), "dX", 16)
     for q in range(10, 16):
         tMa = fire(Y.dma_start(T.MW[q:128:16, :], T.lA[:]), "dMWa", 16)
-    wait(qy, aC, toC, tmLW)
-    tLW = fire(Y.dma_start(T.LW[0:128:16, :], T.lC[:]), "dLW", 16)
-    wait(qc, ton, tcs)
-    for k in range(8):
-        tsk = fire(C.activation(T.SK[:, 128 * k:128 * k + 128], T.ON[:], AF.Copy, scale=T.CS[:, k:k + 1]), "sk")
+    wait(qy, aC, toC)
+    for q in range(16):
+        tLW = fire(Y.dma_start(T.LW[q:128:16, :], T.lC[:]), "dLW", 16)
 
-    wait(qv, tow, tz0, tz1, tPW)
+    wait(qv, tow, tz0, tPW)
 
     def pick(h):
         return fire(V.tensor_tensor(T.GB[:, 512 * h:512 * h + 512], T.PW[:].indirect(T.OW[:, 32 * h:32 * h + 32]),
                                     T.ZM[:, 512 * h:512 * h + 512], A.mult), "gp%d" % h)
 
     tg = {0: pick(0)}
+    wait(qv, tz1)
+    tg[1] = pick(1)
     wait(qv, tX)
     tlo = fire(V.tensor_scalar(T.L0[:], T.X0[:], 2047, None, A.bitwise_and), "lo")
-    thi = fire(V.tensor_scalar(T.HI[:, 0:16], T.X0[:], 11, None, A.arith_shift_right), "hi")
+    thi = fire(V.tensor_scalar(T.H0[:], T.X0[:], 11, None, A.arith_shift_right), "hi")
     wait(qv, tlo)
     tof = fire(V.tensor_copy(T.OF[:, 0:16], T.L0[:]), "of")
-    tsl = fire(V.tensor_copy(T.SL[:, 0:16], T.L0[:]), "sl")
     wait(qv, thi)
-    thh = fire(V.tensor_scalar(T.HH[:, 0:16], T.HI[:, 0:16], 2048, None, A.add), "hh")
+    thh = fire(V.tensor_scalar(T.HH[:, 0:16], T.H0[:], 2048, None, A.add), "hh")
     tcp, tsq, banks = {}, {}, []
 
     def seq(j):
-        wait(qt, tsk, tz0, tz1, tg[j // 8])
         n = len(banks)
-        if n >= 4:
-            wait(qt, tcp[banks[n - 4]])
+        if n >= 6:
+            wait(qt, tcp[banks[n - 6]])
         banks.append(j)
+        bank = ("QB0", "QB1", "QB2", "QB3", "CQ", "CP")[n % 6]
         h, k = j // 8, j % 8
-        m = TE.matmul(T["QB%d" % (n % 4)][:], T.SK[:, 128 * k:128 * k + 128], T.GB[:, 512 * h:512 * h + 512], True, True)
-        tsq[j] = (n % 4, fire(m, "sq%d" % j))
+        wait(qt, tsk, tow, tz0, tz1, tg[h])
+        sel = T.SK[:, 128 * k:128 * k + 512:4] if h else T.SK[:, 128 * k:128 * k + 128]
+        m = TE.matmul(T[bank][:], sel, T.GB[:, 512 * h:512 * h + 512], True, True)
+        tsq[j] = (bank, fire(m, "sq%d" % j))
 
     def cpy(j):
         wait(qc, tsq[j][1])
-        tcp[j] = fire(C.activation(T.SQ[:, PAD + 512 * j:PAD + 512 * j + 512], T["QB%d" % tsq[j][0]][:], AF.Copy), "cp%d" % j)
+        b = T[tsq[j][0]]
+        if j < 8:
+            tcp[j] = fire(C.activation(T.SQ[:, PAD + 512 * j:PAD + 512 * j + 512], b[:], AF.Copy, bias=-256.0), "cp%d" % j)
+            return
+        R = T["R%d" % j]
+        tcp[j] = fire(C.activation(R[:], b[:], AF.Copy, bias=-256.0), "cp%d" % j)
+        wait(qy, tcp[j])
+        for i in range(4):
+            k = PAD + 512 * (j + i)
+            for u in range(4):
+                late[j] = fire(Y.dma_start(T.SQ[32 * u:32 * u + 32, k:k + 512], R[32 * i:32 * i + 32, :]), "dR%d" % j, 16)
 
+    late = {}
     for j in range(6):
         seq(j)
+    for j in range(2):
         cpy(j)
-    tg[1] = pick(1)
 
-    tlg, tlc, tsy, tii = {}, {}, {}, {}
+    tlg, tlc, tsy, tii, tk = {}, {}, {}, {}, {}
 
-    def letters(s, tok):
-        wait(qc, tok, tLW)
+    def letters(s):
+        wait(qc, toff[s], tLW)
         tlg[s] = fire(C.activation(T.LG[:, 256 * s:256 * s + 256], T.LW[:].indirect(T.OF[:, 16 * s:16 * s + 16]), AF.Copy), "lg")
 
     def compact(a, b, lo=0, hi=16):
-        wait(qt, tlg[b - 1], tes, tow)
+        wait(qt, tlg[b - 1], tes, tow, tcp[4], tcp[5])
         CP = T.CQ if a else T.CP
         for q in range(lo, hi):
             m = TE.matmul(CP[:, 0:16 * (b - a)], T.ES[:, 15 - q:143 - q], T.LG[:, 256 * a + q:256 * b:16], q == 0, q == 15)
@@ -246,88 +284,106 @@ def rank_program(g, core, T, topo):
         wait(qc, tlc[a])
         tsy[a] = fire(C.activation(T.SY[:, 16 * a:16 * b], (T.CQ if a else T.CP)[:, 0:16 * (b - a)], AF.Copy), "sy")
 
+    def lookup(out, win, off, s, cv, tok, bias, nv, nc, scan, M, ns, gap):
+        k = 16 * cv
+        if cv < 16:
+            wait(qc, *tok)
+            tc = fire(C.activation(out[:, k:256], win.indirect(off[:, 16 * s + cv:16 * s + 16]), AF.Identity, bias=bias), nc)
+        wait(qv, *tok)
+        tv = fire(V.tensor_scalar(out[:, 0:k], win.indirect(off[:, 16 * s:16 * s + cv]), bias, None, A.add), nv)
+        gap()
+        wait(qv, tv)
+        t = fire(V.tensor_tensor_scan(scan[:, 0:k], M[:, 0:k], out[:, 0:k], 0.0, A.add, A.max), ns)
+        if cv < 16:
+            wait(qv, tc)
+            t = fire(V.tensor_tensor_scan(scan[:, k:256], M[:, k:256], out[:, k:256], 0.0, A.add, A.max), ns)
+        return t
+
     toff = {0: tof}
+    slot, tsl = T.L0[:], tlo
     for s in range(S):
         c = slice(16 * s, 16 * s + 16)
         n = slice(16 * s + 16, 16 * s + 32)
-        MA, SA, MB, SB = T["MA%d" % s], T["SA%d" % s], T["MB%d" % s], T["SB%d" % s]
+        d = slice(32 * s, 32 * s + 32)
+        MA, SA, GM, SB = T["MA%d" % s], T["SA%d" % s], T["GM%d" % s], T["SB%d" % s]
+
+        def gap1():
+            wait(qv, tsl, thh)
+            tk["aa"] = fire(V.tensor_tensor(T.AA[:, c], T.HH[:, c], slot, A.add), "aa")
+
+        wait(qv, tme)
+        tsa = lookup(MA, T.MW[:], T.OF, s, CV[s], [toff[s], tMa, tMb, tkg], T.EB[:, 0:1], "ga", "gc", SA, T.ME, "sa", gap1)
         if s == 0:
-            wait(qv, tMa, tMb, tmk)
-        wait(qv, toff[s])
-        tga = fire(V.tensor_tensor(MA[:], T.MW[:].indirect(T.OF[:, c]), T.MK[:], A.mult), "ga")
-        wait(qv, tsl)
-        taa = fire(V.tensor_tensor(T.AA[:, c], T.HI[:, c], T.SL[:, c], A.add), "aa")
-        wait(qv, tga, tk6b)
-        tsa = fire(V.tensor_tensor_scan(SA[:], T.K16[:], MA[:], 0.0, A.mult, A.add), "sa")
-        if s:
-            thh = fire(V.tensor_scalar(T.HH[:, c], T.HI[:, c], 2048, None, A.add), "hh")
+            for j in range(2, 6):
+                cpy(j)
         wait(qv, tsa)
         e = SA[:, 15:256:16]
-        tff = fire(V.tensor_scalar(T.FF[:, c], e, 1.0 / 2048, -1023.5 / 2048, A.mult, A.add), "ff")
-        wait(qv, taa)
-        tqq = fire(V.tensor_tensor(T.QQ[:, c], e, T.AA[:, c], A.subtract), "qq")
+        tff = fire(V.tensor_scalar(T.FF[:, c], e, 1.0 / 2048, -3 - 1023.5 / 2048, A.mult, A.add), "ff")
+        wait(qv, tk["aa"])
+        tq4 = fire(V.tensor_tensor(T.Q4[:, c], e, T.AA[:, c], A.subtract), "q4")
         wait(qv, tff, thh)
         tpp = fire(V.tensor_tensor(T.PP[:, c], T.FF[:, c], T.HH[:, c], A.mult), "pp")
+        wait(qv, tq4)
+        tqq = fire(V.tensor_scalar(T.QQ[:, c], T.Q4[:, c], 4096, None, A.subtract), "qq")
+        wait(qv, tpp, trz)
+        trr = fire(V.tensor_tensor(T.RR[:, 32 * s:32 * s + 16], T.PP[:, c], T.Q4[:, c], A.is_lt), "rr")
         wait(qv, tqq)
-        tq4 = fire(V.tensor_scalar(T.Q4[:, c], T.QQ[:, c], 4096, None, A.add), "q4")
-        wait(qv, tpp, tq4)
-        trr = fire(V.tensor_tensor(T.RR[:, c], T.PP[:, c], T.Q4[:, c], A.is_lt), "rr")
         txx = fire(V.tensor_tensor(T.XX[:, c], T.PP[:, c], T.QQ[:, c], A.subtract), "xx")
         wait(qv, trr, ton)
-        tii[s] = fire(V.tensor_tensor_scan(T.II[:, c], T.ON[:, 0:16], T.RR[:, c], 0.0, A.mult, A.add), "ii")
-        tm2 = fire(V.tensor_scalar(T.MM[:, c], T.RR[:, c], 255, 1, A.mult, A.add), "m2")
-        tnb = fire(V.tensor_scalar(T.NB[:, c], T.RR[:, c], BIG, PAD - 1 - BIG, A.mult, A.add), "nb")
-        PR = T["PR%d" % (s % 2)]
-        wait(qt, tsu)
+        tii[s] = fire(V.tensor_tensor_scan(T.II[:, d], T.ON[:, 0:32], T.RR[:, d], 0.0, A.mult, A.add), "ii")
+        tm2 = fire(V.tensor_scalar(T.MM[:, c], T.RR[:, 32 * s:32 * s + 16], 255, 1, A.mult, A.add), "m2")
+        if s == 3:
+            letters(3)
+            collect(0, 3)
+        PR = T["PR%d" % (s % 2)][:, c]
+        wait(qt, tsu, tig, tme, tmb)
         if s:
             wait(qt, tii[s - 1])
         for b in range(s):
-            TE.matmul(PR[:, s:s + 1], T.ON[:], T.II[:, 16 * b + 15:16 * b + 16], b == 0, False)
+            TE.matmul(PR, T.ON[:], T.II[:, 32 * b + 16:32 * b + 32], b == 0, False)
         if s == 3:
-            letters(3, toff[3])
             compact(3, 4, 0, 4)
+        wait(qt, trr)
+        TE.matmul(PR, T.IG[:], T.RR[:, 32 * s:32 * s + 16], s == 0, False)
         wait(qt, tii[s])
-        tpf = fire(TE.matmul(PR[:, s:s + 1], T.SU[:], T.II[:, 16 * s + 15:16 * s + 16], s == 0, True), "pf")
-        if s in (1, 2):
-            letters(s, toff[s])
-        for j in range(*((6, 11), (11, 14), (14, 16), (0, 0))[s]):
+        TE.matmul(PR, T.IB[:], T.II[:, 32 * s:32 * s + 16], False, False)
+        tpf = fire(TE.matmul(PR, T.SU[:], T.II[:, 32 * s + 16:32 * s + 32], False, True), "pf")
+        for j in ((8, 6, 7, 12), (), (), ())[s]:
             seq(j)
-            cpy(j)
-        if s == 0:
-            letters(0, toff[0])
+        for x in SLOT_A[s]:
+            cpy(x) if x >= 4 else letters(x)
+        wait(qv, tm2, txx)
+        tvv = fire(V.tensor_tensor(T.VV[:, c], T.XX[:, c], T.MM[:, c], A.mult), "vv")
+        wait(qv, tpf)
+        tot = fire(V.tensor_scalar(T.OT[:, c], PR, PAD - 1 - BIG, None, A.add), "ot")
+        wait(qv, tvv)
+        if s < 3:
+            thh = fire(V.tensor_scalar(T.HH[:, n], T.VV[:, c], 1.0 / 2048, 2048 - 1023.5 / 2048, A.mult, A.add), "hh")
+
+        def gap2():
+            if s < 3:
+                tk["dd"] = fire(V.tensor_scalar(T.DD[:, c], T.VV[:, c], 2047, None, A.bitwise_and), "dd")
+
+        wait(qv, tmb)
+        made = [tcp[j] for j in range(min(8, 4 * s + 4))] + [late[j] for j in (8, 12)[:max(0, s - 1)]]
+        tsb = lookup(GM, T.SQ[:, 0:PAD + 2048 * (s + 1)], T.OT, s, CW[s], [tot, tpad, tkg] + made, T.BB[:, 0:1], "gb", "hb",
+                     SB, T.MB, "sb", gap2)
+        for x in SLOT_B[s]:
+            cpy(x) if x >= 4 else letters(x)
         if s == 2:
             compact(0, 3)
-            collect(0, 3)
         if s == 3:
             compact(3, 4, 4, 16)
             collect(3, 4)
-        wait(qv, tm2, txx)
-        tvv = fire(V.tensor_tensor(T.VV[:, c], T.XX[:, c], T.MM[:, c], A.mult), "vv")
-        wait(qv, tnb, tii[s])
-        ti2 = fire(V.tensor_tensor(T.I2[:, c], T.II[:, c], T.NB[:, c], A.add), "i2")
-        if s < 3:
-            wait(qv, tvv)
-            thi = fire(V.tensor_scalar(T.HI[:, n], T.VV[:, c], 1.0 / 2048, -1023.5 / 2048, A.mult, A.add), "hi")
-        wait(qv, ti2, tpf)
-        tot = fire(V.tensor_scalar(T.OT[:, c], T.I2[:, c], PR[:, s:s + 1], None, A.add), "ot")
-        if s < 3:
-            wait(qv, thi)
-            tnh = fire(V.tensor_scalar(T.NH[:, c], T.HI[:, n], -2048, None, A.mult), "nh")
-        wait(qv, tot, tpad, *[tcp[j] for j in range(4 * s + 4)])
-        tgb = fire(V.tensor_tensor(MB[:], T.SQ[:, 0:PAD + 2048 * (s + 1)].indirect(T.OT[:, c]), T.MK[:], A.mult), "gb")
-        if s < 3:
-            wait(qv, tnh)
-            tdd = fire(V.tensor_tensor(T.DD[:, c], T.VV[:, c], T.NH[:, c], A.add), "dd")
-        wait(qv, tgb, tkbb)
-        tsb = fire(V.tensor_tensor_scan(SB[:], T.KB[:], MB[:], 0.0, A.mult, A.add), "sb")
         b = SB[:, 15:256:16]
         if s < 3:
-            wait(qv, tsb, tdd)
+            wait(qv, tsb, tk["dd"])
             tsl = fire(V.tensor_tensor(T.SL[:, n], b, T.DD[:, c], A.add), "sl")
+            slot = T.SL[:, n]
             wait(qv, tsl)
-            toff[s + 1] = fire(V.tensor_copy(T.OF[:, n], T.SL[:, n]), "of")
+            toff[s + 1] = fire(V.tensor_copy(T.OF[:, n], slot), "of")
         else:
-            wait(qv, tsb, tvv)
+            wait(qv, tsb)
             tfn = fire(V.tensor_tensor(T.FN[:], b, T.VV[:, c], A.add), "fn")
 
     half = {0: slice(0, 64), 1: slice(64, 128), 2: slice(0, 128), 3: slice(0, 64)}

import numpy as np
from concourse.bass import DstId, RemoteDMATransfer
from concourse.mybir import dt, AluOpType, AxisListType, ActivationFunctionType

N, S, PAD, BIG = 8, 4, 16, 16384
E22 = 4194304
CV = (8, 6, 6, 6)
CW = (16, 6, 6, 6)
SLOT_A = ((8,), (6, 7), (0, 1), ())
SLOT_B = ((), (12,), (2,), ())

SCRATCH = {
    "pS": ("dram", [8, 128, 2], "int32"), "pA": ("dram", [8, 128, 16], "int32"),
    "pB": ("dram", [8, 128, 8], "int32"), "pC": ("dram", [8, 128, 16], "bfloat16"),
    "lS": ("dram", [8, 128, 2], "int32"), "lA": ("dram", [8, 128, 16], "int32"),
    "lB": ("dram", [8, 128, 8], "int32"), "lC": ("dram", [8, 128, 16], "bfloat16"),
    "rY": ("dram", [8, 128, 4], "float32"), "rZ": ("dram", [8, 128, 2], "float32"), "rF": ("dram", [8, 128, 4], "float32"),
    "lY": ("dram", [8, 128, 4], "float32"), "lZ": ("dram", [8, 128, 2], "float32"), "lF": ("dram", [8, 128, 4], "float32"),
    "CW": ("sbuf", [128, 128], "int32"), "CN": ("sbuf", [128, 128], "bfloat16"),
    "MW": ("sbuf", [128, 2048], "int32"), "PW": ("sbuf", [128, 512], "int32"),
    "LW": ("sbuf", [128, 2048], "bfloat16"), "SQ": ("sbuf", [128, PAD + 8192], "bfloat16"),
    "R8": ("sbuf", [128, 512], "bfloat16"), "R12": ("sbuf", [128, 512], "bfloat16"),
    "BI": ("sbuf", [128, 128], "int32"), "BJ": ("sbuf", [128, 128], "int32"), "BF": ("sbuf", [128, 128], "float32"),
    "OW": ("sbuf", [128, 64], "uint16"), "P8": ("sbuf", [128, 1024], "int32"),
    "PB": ("sbuf", [128, 1024], "bfloat16"), "ZM": ("sbuf", [128, 1024], "bfloat16"), "GB": ("sbuf", [128, 1024], "bfloat16"),
    "IT": ("sbuf", [128, 160], "int32"), "IA": ("sbuf", [128, 16], "int32"), "QI": ("sbuf", [128, 8], "int32"),
    "KI": ("sbuf", [128, 8], "int32"), "GI": ("sbuf", [128, 128], "int32"), "GS": ("sbuf", [128, 128], "bfloat16"),
    "QA": ("sbuf", [128, 8], "int32"), "QD": ("sbuf", [128, 8], "int32"), "QF": ("sbuf", [128, 8], "float32"),
    "PF": ("sbuf", [128, 8], "float32"), "QL": ("sbuf", [128, 8], "float32"),
    "EB": ("sbuf", [128, 8], "float32"), "BB": ("sbuf", [128, 8], "float32"), "KE": ("sbuf", [128, 8], "float32"),
    "M0": ("sbuf", [128, 16], "float32"), "M1": ("sbuf", [128, 16], "float32"), "M2": ("sbuf", [128, 16], "bfloat16"),
    "ME": ("sbuf", [128, 256], "float32"), "MB": ("sbuf", [128, 256], "bfloat16"),
    "ON": ("sbuf", [128, 128], "bfloat16"), "SU": ("sbuf", [128, 128], "bfloat16"), "ES": ("sbuf", [128, 144], "bfloat16"),
    "ID": ("sbuf", [128, 128], "float32"), "IB": ("sbuf", [128, 128], "bfloat16"), "IG": ("sbuf", [128, 128], "bfloat16"),
    "CS": ("sbuf", [128, 8], "float32"), "SK": ("sbuf", [128, 1024], "bfloat16"),
    "X0": ("sbuf", [128, 16], "int32"), "L0": ("sbuf", [128, 16], "int32"), "H0": ("sbuf", [128, 16], "int32"),
    "OF": ("sbuf", [128, 64], "uint16"), "OT": ("sbuf", [128, 64], "uint16"),
    "HH": ("sbuf", [128, 64], "int32"), "SL": ("sbuf", [128, 64], "float32"),
    "AA": ("sbuf", [128, 64], "float32"), "FF": ("sbuf", [128, 64], "int32"),
    "Q4": ("sbuf", [128, 64], "float32"), "QQ": ("sbuf", [128, 64], "float32"), "PP": ("sbuf", [128, 64], "float32"),
    "RR": ("sbuf", [128, 128], "bfloat16"), "II": ("sbuf", [128, 128], "bfloat16"), "XX": ("sbuf", [128, 64], "float32"),
    "MM": ("sbuf", [128, 64], "float32"), "VV": ("sbuf", [128, 64], "int32"), "DD": ("sbuf", [128, 64], "int32"),
    "LG": ("sbuf", [128, 1024], "bfloat16"), "SY": ("sbuf", [128, 64], "float32"), "FN": ("sbuf", [128, 16], "float32"),
    "PR0": ("psum", [128, 512], "float32"), "PR1": ("psum", [128, 512], "float32"),
    "CP": ("psum", [128, 512], "float32"), "CQ": ("psum", [128, 512], "float32"),
}
for _s in range(S):
    SCRATCH["MA%d" % _s] = ("sbuf", [128, 256], "float32")
    SCRATCH["SA%d" % _s] = ("sbuf", [128, 256], "float32")
    SCRATCH["GM%d" % _s] = ("sbuf", [128, 256], "bfloat16")
    SCRATCH["SB%d" % _s] = ("sbuf", [128, 256], "bfloat16")
for _b in range(4):
    SCRATCH["QB%d" % _b] = ("psum", [128, 512], "float32")

SEMAPHORES = (["aS", "aA", "aB", "aC", "aY", "aZ", "aF", "sent"]
              + ["dB", "dC", "wC", "nC", "dS", "dA", "oS", "oA", "oB", "oC", "dPl", "dP8", "dX", "dPW", "pi", "dMWa", "dMWb", "dLW"]
              + ["dY", "dZ", "dF3", "dFl", "oY", "oZ", "oF3", "oFl", "out1", "out2"]
              + ["dR8", "dR12", "m2b", "mm", "pb1", "kg", "it", "qi", "ki", "gi", "gs", "qa", "qd", "qf", "pF", "pb", "za", "zt",
                 "zm0", "zm1", "ia", "ql", "kf", "m0", "m1", "me", "on", "su", "es", "ez", "id", "igb", "cs", "sk", "pad", "rz",
                 "bj", "bf", "tp", "ow", "gp0", "gp1"]
              + ["sq%d" % j for j in range(13)] + ["cp%d" % j for j in range(13)]
              + ["lo", "hi", "hh", "of", "sl", "ga", "gc", "aa", "sa", "ff", "q4", "pp", "qq", "rr", "ii", "pf", "xx", "m2",
                 "vv", "ot", "gb", "hb", "dd", "sb", "fn", "lg", "lc0", "lc3", "sy"])


def rank_program(g, core, T, topo):
    me = T.rank_of(core)
    if me is None:
        return
    A, AF = AluOpType, ActivationFunctionType
    V, C, TE, Y = g.vector, g.scalar, g.tensor, g.sync
    count, known, seen = {}, {}, {}

    def fire(ins, name, n=1):
        ins.then_inc(T.sem[name], n)
        count[name] = count.get(name, 0) + n
        return (name, count[name])

    def wait(q, *tokens):
        for name, val in tokens:
            k = (q[0], name)
            if known.get(k, 0) < val:
                known[k] = val
                seen[name] = max(seen.get(name, 0), val)
                q[1].wait_ge(T.sem[name], val)

    qg, qv, qc, qt, qy = ("g", g), ("v", V), ("c", C), ("t", TE), ("y", Y)

    engine = {}
    for d in T.cores:
        if d != core and topo.chip(d) != topo.chip(core):
            e = topo.engines(core, d)
            engine[d] = [x for x in e[0::2] + e[1::2] if x not in engine.values()][0]
    for d in T.cores:
        if d != core and topo.chip(d) == topo.chip(core):
            engine[d] = [x for x in topo.engines(core, d)[::-1] if x not in engine.values()][0]

    def send(src, dst, sem):
        tr = []
        for d in engine:
            rid, pid, _ = topo.addr(d)
            tr.append(RemoteDMATransfer(dst_ids=[DstId(rid=rid, pnc=pid)], dma_engine_mask=1 << engine[d], remote_sem=T.sem[sem],
                                        srcs=[T[src][T.rank_of(d)]], dsts=[T[dst][me]], alu_op=0))
        g.remote_dma_fused(tr, local_sem=T.sem.sent)
        count["sent"] = count.get("sent", 0) + len(tr)
        count[sem] = count.get(sem, 0) + len(tr)
        return (sem, len(tr))

    m0 = slice(16 * me, 16 * me + 16)
    tdB = fire(C.dma_start(T.pB[:], T.stock[:]), "dB", 16)
    tdA = fire(Y.dma_start(T.pA[:], T.models[:]), "dA", 16)
    tdS = fire(Y.dma_start(T.pS[:], T.states[:]), "dS", 16)
    twC = fire(C.dma_start(T.CW[:], T.letters[:]), "wC", 16)
    for h in range(2):
        tP8 = fire(Y.dma_start(T.P8[0:8, 512 * h:512 * h + 512], T.places[me, 4096 * h:4096 * h + 4096]), "dP8", 16)
    toA = fire(C.dma_start(T.lA[me], T.models[me]), "oA", 16)
    toS = fire(Y.dma_start(T.lS[me], T.states[me]), "oS", 16)
    toB = fire(C.dma_start(T.lB[me], T.stock[me]), "oB", 16)
    for h in range(2):
        for k in range(8):
            t = 4096 * h + 512 * k
            tPl = fire((Y if k % 2 else C).dma_start(T.BI[32 * h:32 * h + 32, 16 * k:16 * k + 16], T.places[me, t:t + 512]), "dPl", 16)
    tit = fire(g.iota(T.IT[:], [[1, 160]], -15, -1), "it")
    tgi = fire(g.iota(T.GI[0:8, :], [[1, 8], [0, 16]], 0, -1), "gi")
    tqi = fire(g.iota(T.QI[:], [[0, 8]], 0, 1), "qi")
    tki = fire(g.iota(T.KI[:], [[1, 8]], 0, 0), "ki")
    wait(qg, tdB)
    aB = send("pB", "lB", "aB")
    wait(qg, tdA)
    aA = send("pA", "lA", "aA")
    wait(qg, tdS)
    aS = send("pS", "lS", "aS")

    ton = fire(V.memset(T.ON[:], 1.0), "on")
    trz = fire(V.memset(T.RR[:], 0.0), "rz")
    tpad = fire(V.memset(T.SQ[:, 0:PAD], -256.0), "pad")
    wait(qv, tit)
    tid = fire(V.tensor_scalar(T.ID[:], T.IT[:, 15:143], 0, None, A.is_equal), "id")
    tia = fire(V.tensor_scalar(T.IA[:], T.IT[:, 15:31], 15, None, A.bitwise_and), "ia")
    wait(qv, tgi, tqi, tki)
    tgs = fire(V.tensor_scalar(T.GS[0:8, :], T.GI[0:8, :], 0, None, A.is_equal), "gs")
    tqa = fire(V.tensor_scalar(T.QA[:], T.QI[:], 15, None, A.bitwise_and), "qa")
    tqd = fire(V.tensor_scalar(T.QD[:], T.QI[:], 4, None, A.arith_shift_right), "qd")
    wait(qv, tia)
    tm0 = fire(V.tensor_scalar(T.M0[:], T.IA[:], 0, -2, A.is_equal, A.mult), "m0")
    tm1 = fire(V.tensor_scalar(T.M1[:], T.IA[:], 1, None, A.is_equal), "m1")
    wait(qv, tqa, tqd)
    tql = fire(V.tensor_scalar(T.QL[:], T.QA[:], 15, None, A.is_equal), "ql")
    tpF = fire(V.tensor_copy(T.PF[:], T.QD[:]), "pF")
    wait(qv, tm0, tm1)
    tm2 = fire(V.tensor_tensor(T.M2[:], T.M0[:], T.M1[:], A.add), "m2b")
    tqf = fire(V.tensor_scalar(T.QF[:], T.QA[:], 144, None, A.add), "qf")
    wait(qv, tpF)
    tcs = fire(V.tensor_scalar(T.CS[:], T.KI[:], T.PF[:, 0:1], None, A.is_equal), "cs")
    tke = fire(V.tensor_scalar(T.KE[:], T.QA[:], 0, None, A.is_equal), "kf")
    tsu = fire(V.tensor_scalar(T.SU[:], T.IT[:, 15:143], 0, None, A.is_gt), "su")
    tez = fire(V.memset(T.ES[:], 0.0), "ez")
    wait(qc, tid)
    tib = fire(C.activation(T.IB[:], T.ID[:], AF.Copy), "igb")
    wait(qc, tql)
    fire(C.activation(T.EB[:], T.QL[:], AF.Copy, scale=float(E22), bias=float(6144 - E22)), "kg")
    tkg = fire(C.activation(T.BB[:], T.QL[:], AF.Copy, scale=256.0), "kg")
    wait(qc, ton, tcs)
    for k in range(8):
        tsk = fire(C.activation(T.SK[:, 128 * k:128 * k + 128], T.ON[:], AF.Copy, scale=T.CS[:, k:k + 1]), "sk")
    tig = fire(C.activation(T.IG[:], T.ID[:], AF.Copy, scale=float(BIG)), "igb")
    wait(qc, tke, tez)
    tes = fire(C.activation(T.ES[:, 15:143], T.ID[:], AF.Copy, scale=T.KE[:, 0:1]), "es")
    wait(qt, tib, tm2)
    for q in range(16):
        m = TE.matmul(T.PR1[:, 16 * q:16 * q + 16], T.IB[:], T.M2[:], True, True)
    tmm = fire(m, "mm")
    wait(qv, tP8)
    tpb = fire(V.tensor_scalar(T.PB[0:8, 0:512], T.P8[0:8, 0:512], 1.0 / 512, 143.501, A.mult, A.add), "pb")
    wait(qv, tPl)
    tbj = fire(V.tensor_scalar(T.BJ[0:64, :], T.BI[0:64, :], 511, None, A.bitwise_and), "bj")
    wait(qv, twC)
    tnC = fire(V.tensor_copy(T.CN[:], T.CW[:]), "nC")
    wait(qv, tbj)
    tbf = fire(V.tensor_copy(T.BF[0:64, :], T.BJ[0:64, :]), "bf")
    tpc = fire(V.tensor_scalar(T.PB[0:8, 512:1024], T.P8[0:8, 512:1024], 1.0 / 512, 143.501, A.mult, A.add), "pb1")
    wait(qt, tgs, tpb)
    tza = fire(TE.matmul(T.QB0[:], T.GS[0:8, :], T.PB[0:8, 0:512], True, True), "za")
    wait(qt, tid, tbf)
    ttp = fire(TE.transpose(T.CP[:, 64:128], T.BF[0:64, :], T.ID[0:64, 0:64]), "tp")
    wait(qt, tpc)
    tzt = fire(TE.matmul(T.QB1[:], T.GS[0:8, :], T.PB[0:8, 512:1024], True, True), "zt")
    wait(qv, tza, tqf)
    tz0 = fire(V.tensor_scalar(T.ZM[:, 0:512], T.QB0[:], T.QF[:, 0:1], None, A.is_equal), "zm0")
    wait(qv, ttp)
    tow = fire(V.tensor_copy(T.OW[:], T.CP[:, 64:128]), "ow")
    wait(qv, tzt)
    tz1 = fire(V.tensor_scalar(T.ZM[:, 512:1024], T.QB1[:], T.QF[:, 0:1], None, A.is_equal), "zm1")

    wait(qc, tmm)
    tme = fire(C.activation(T.ME[:], T.PR1[:, 0:256], AF.Copy, scale=float(E22)), "me")
    tmb = fire(C.activation(T.MB[:], T.PR1[:, 0:256], AF.Copy, scale=256.0), "igb")
    wait(qc, tnC)
    tdC = fire(C.dma_start(T.pC[:], T.CN[:]), "dC", 16)
    toC = fire(C.dma_start(T.lC[me], T.CN[m0, :]), "oC", 16)
    wait(qg, tdC)
    aC = send("pC", "lC", "aC")
    wait(qy, aB, toB)
    for k in range(8):
        tPW = fire(Y.dma_start(T.PW[16 * k:16 * k + 16, :], T.lB[:]), "dPW", 16)
    Y.sem_inc(T.sem.pi, 1)
    count["pi"] = 1
    wait(qc, aA, toA, ("pi", 1))
    for q in range(10):
        tMb = fire(C.dma_start(T.MW[q:128:16, :], T.lA[:]), "dMWb", 16)
    wait(qy, aA, aS, toA, toS)
    tX = fire(Y.dma_start(T.X0[:], T.lS[:]), "dX", 16)
    for q in range(10, 16):
        tMa = fire(Y.dma_start(T.MW[q:128:16, :], T.lA[:]), "dMWa", 16)
    wait(qy, aC, toC)
    for q in range(16):
        tLW = fire(Y.dma_start(T.LW[q:128:16, :], T.lC[:]), "dLW", 16)

    wait(qv, tow, tz0, tPW)

    def pick(h):
        return fire(V.tensor_tensor(T.GB[:, 512 * h:512 * h + 512], T.PW[:].indirect(T.OW[:, 32 * h:32 * h + 32]),
                                    T.ZM[:, 512 * h:512 * h + 512], A.mult), "gp%d" % h)

    tg = {0: pick(0)}
    wait(qv, tz1)
    tg[1] = pick(1)
    wait(qv, tX)
    tlo = fire(V.tensor_scalar(T.L0[:], T.X0[:], 2047, None, A.bitwise_and), "lo")
    thi = fire(V.tensor_scalar(T.H0[:], T.X0[:], 11, None, A.arith_shift_right), "hi")
    wait(qv, tlo)
    tof = fire(V.tensor_copy(T.OF[:, 0:16], T.L0[:]), "of")
    wait(qv, thi)
    thh = fire(V.tensor_scalar(T.HH[:, 0:16], T.H0[:], 2048, None, A.add), "hh")
    tcp, tsq, banks = {}, {}, []

    def seq(j):
        n = len(banks)
        if n >= 6:
            wait(qt, tcp[banks[n - 6]])
        banks.append(j)
        bank = ("QB0", "QB1", "QB2", "QB3", "CQ", "CP")[n % 6]
        h, k = j // 8, j % 8
        wait(qt, tsk, tow, tz0, tz1, tg[h])
        sel = T.SK[:, 128 * k:128 * k + 512:4] if h else T.SK[:, 128 * k:128 * k + 128]
        m = TE.matmul(T[bank][:], sel, T.GB[:, 512 * h:512 * h + 512], True, True)
        tsq[j] = (bank, fire(m, "sq%d" % j))

    def cpy(j):
        wait(qc, tsq[j][1])
        b = T[tsq[j][0]]
        if j < 8:
            tcp[j] = fire(C.activation(T.SQ[:, PAD + 512 * j:PAD + 512 * j + 512], b[:], AF.Copy, bias=-256.0), "cp%d" % j)
            return
        R = T["R%d" % j]
        tcp[j] = fire(C.activation(R[:], b[:], AF.Copy, bias=-256.0), "cp%d" % j)
        wait(qy, tcp[j])
        for i in range(4):
            k = PAD + 512 * (j + i)
            for u in range(4):
                late[j] = fire(Y.dma_start(T.SQ[32 * u:32 * u + 32, k:k + 512], R[32 * i:32 * i + 32, :]), "dR%d" % j, 16)

    late = {}
    for j in range(6):
        seq(j)
    for j in range(2):
        cpy(j)

    tlg, tlc, tsy, tii, tk = {}, {}, {}, {}, {}

    def letters(s):
        wait(qc, toff[s], tLW)
        tlg[s] = fire(C.activation(T.LG[:, 256 * s:256 * s + 256], T.LW[:].indirect(T.OF[:, 16 * s:16 * s + 16]), AF.Copy), "lg")

    def compact(a, b, lo=0, hi=16):
        wait(qt, tlg[b - 1], tes, tow, tcp[4], tcp[5])
        CP = T.CQ if a else T.CP
        for q in range(lo, hi):
            m = TE.matmul(CP[:, 0:16 * (b - a)], T.ES[:, 15 - q:143 - q], T.LG[:, 256 * a + q:256 * b:16], q == 0, q == 15)
        if hi == 16:
            tlc[a] = fire(m, "lc%d" % a)

    def collect(a, b):
        wait(qc, tlc[a])
        tsy[a] = fire(C.activation(T.SY[:, 16 * a:16 * b], (T.CQ if a else T.CP)[:, 0:16 * (b - a)], AF.Copy), "sy")

    def lookup(out, win, off, s, cv, tok, bias, nv, nc, scan, M, ns, gap):
        k = 16 * cv
        if cv < 16:
            wait(qc, *tok)
            tc = fire(C.activation(out[:, k:256], win.indirect(off[:, 16 * s + cv:16 * s + 16]), AF.Identity, bias=bias), nc)
        wait(qv, *tok)
        tv = fire(V.tensor_scalar(out[:, 0:k], win.indirect(off[:, 16 * s:16 * s + cv]), bias, None, A.add), nv)
        gap()
        wait(qv, tv)
        t = fire(V.tensor_tensor_scan(scan[:, 0:k], M[:, 0:k], out[:, 0:k], 0.0, A.add, A.max), ns)
        if cv < 16:
            wait(qv, tc)
            t = fire(V.tensor_tensor_scan(scan[:, k:256], M[:, k:256], out[:, k:256], 0.0, A.add, A.max), ns)
        return t

    toff = {0: tof}
    slot, tsl = T.L0[:], tlo
    for s in range(S):
        c = slice(16 * s, 16 * s + 16)
        n = slice(16 * s + 16, 16 * s + 32)
        d = slice(32 * s, 32 * s + 32)
        MA, SA, GM, SB = T["MA%d" % s], T["SA%d" % s], T["GM%d" % s], T["SB%d" % s]

        def gap1():
            wait(qv, tsl, thh)
            tk["aa"] = fire(V.tensor_tensor(T.AA[:, c], T.HH[:, c], slot, A.add), "aa")

        wait(qv, tme)
        tsa = lookup(MA, T.MW[:], T.OF, s, CV[s], [toff[s], tMa, tMb, tkg], T.EB[:, 0:1], "ga", "gc", SA, T.ME, "sa", gap1)
        if s == 0:
            for j in range(2, 6):
                cpy(j)
        wait(qv, tsa)
        e = SA[:, 15:256:16]
        tff = fire(V.tensor_scalar(T.FF[:, c], e, 1.0 / 2048, -3 - 1023.5 / 2048, A.mult, A.add), "ff")
        wait(qv, tk["aa"])
        tq4 = fire(V.tensor_tensor(T.Q4[:, c], e, T.AA[:, c], A.subtract), "q4")
        wait(qv, tff, thh)
        tpp = fire(V.tensor_tensor(T.PP[:, c], T.FF[:, c], T.HH[:, c], A.mult), "pp")
        wait(qv, tq4)
        tqq = fire(V.tensor_scalar(T.QQ[:, c], T.Q4[:, c], 4096, None, A.subtract), "qq")
        wait(qv, tpp, trz)
        trr = fire(V.tensor_tensor(T.RR[:, 32 * s:32 * s + 16], T.PP[:, c], T.Q4[:, c], A.is_lt), "rr")
        wait(qv, tqq)
        txx = fire(V.tensor_tensor(T.XX[:, c], T.PP[:, c], T.QQ[:, c], A.subtract), "xx")
        wait(qv, trr, ton)
        tii[s] = fire(V.tensor_tensor_scan(T.II[:, d], T.ON[:, 0:32], T.RR[:, d], 0.0, A.mult, A.add), "ii")
        tm2 = fire(V.tensor_scalar(T.MM[:, c], T.RR[:, 32 * s:32 * s + 16], 255, 1, A.mult, A.add), "m2")
        if s == 3:
            letters(3)
            collect(0, 3)
        PR = T["PR%d" % (s % 2)][:, c]
        wait(qt, tsu, tig, tme, tmb)
        if s:
            wait(qt, tii[s - 1])
        for b in range(s):
            TE.matmul(PR, T.ON[:], T.II[:, 32 * b + 16:32 * b + 32], b == 0, False)
        if s == 3:
            compact(3, 4, 0, 4)
        wait(qt, trr)
        TE.matmul(PR, T.IG[:], T.RR[:, 32 * s:32 * s + 16], s == 0, False)
        wait(qt, tii[s])
        TE.matmul(PR, T.IB[:], T.II[:, 32 * s:32 * s + 16], False, False)
        tpf = fire(TE.matmul(PR, T.SU[:], T.II[:, 32 * s + 16:32 * s + 32], False, True), "pf")
        for j in ((8, 6, 7, 12), (), (), ())[s]:
            seq(j)
        for x in SLOT_A[s]:
            cpy(x) if x >= 4 else letters(x)
        wait(qv, tm2, txx)
        tvv = fire(V.tensor_tensor(T.VV[:, c], T.XX[:, c], T.MM[:, c], A.mult), "vv")
        wait(qv, tpf)
        tot = fire(V.tensor_scalar(T.OT[:, c], PR, PAD - 1 - BIG, None, A.add), "ot")
        wait(qv, tvv)
        if s < 3:
            thh = fire(V.tensor_scalar(T.HH[:, n], T.VV[:, c], 1.0 / 2048, 2048 - 1023.5 / 2048, A.mult, A.add), "hh")

        def gap2():
            if s < 3:
                tk["dd"] = fire(V.tensor_scalar(T.DD[:, c], T.VV[:, c], 2047, None, A.bitwise_and), "dd")

        wait(qv, tmb)
        made = [tcp[j] for j in range(min(8, 4 * s + 4))] + [late[j] for j in (8, 12)[:max(0, s - 1)]]
        tsb = lookup(GM, T.SQ[:, 0:PAD + 2048 * (s + 1)], T.OT, s, CW[s], [tot, tpad, tkg] + made, T.BB[:, 0:1], "gb", "hb",
                     SB, T.MB, "sb", gap2)
        for x in SLOT_B[s]:
            cpy(x) if x >= 4 else letters(x)
        if s == 2:
            compact(0, 3)
        if s == 3:
            compact(3, 4, 4, 16)
            collect(3, 4)
        b = SB[:, 15:256:16]
        if s < 3:
            wait(qv, tsb, tk["dd"])
            tsl = fire(V.tensor_tensor(T.SL[:, n], b, T.DD[:, c], A.add), "sl")
            slot = T.SL[:, n]
            wait(qv, tsl)
            toff[s + 1] = fire(V.tensor_copy(T.OF[:, n], slot), "of")
        else:
            wait(qv, tsb)
            tfn = fire(V.tensor_tensor(T.FN[:], b, T.VV[:, c], A.add), "fn")

    half = {0: slice(0, 64), 1: slice(64, 128), 2: slice(0, 128), 3: slice(0, 64)}

    def put(s, out, own, so, sw):
        wait(qy, tsy[3 if s == 3 else 0])
        c = slice(16 * s, 16 * s + 16)
        a = fire(Y.dma_start(out[:, half[s], :], T.SY[:, c]), so, 16)
        b = fire(Y.dma_start(own[me, half[s], :], T.SY[m0, c]), sw, 16)
        return a, b

    put(0, T.rY, T.lY, "dY", "oY")
    a, oY = put(1, T.rY, T.lY, "dY", "oY")
    wait(qg, a)
    aY = send("rY", "lY", "aY")
    a, oZ = put(2, T.rZ, T.lZ, "dZ", "oZ")
    wait(qg, a)
    aZ = send("rZ", "lZ", "aZ")
    a, oF3 = put(3, T.rF, T.lF, "dF3", "oF3")
    wait(qc, tfn)
    b = fire(C.dma_start(T.rF[:, 64:128, :], T.FN[:]), "dFl", 16)
    oFl = fire(C.dma_start(T.lF[me, 64:128, :], T.FN[m0, :]), "oFl", 16)
    wait(qg, a, b)
    aF = send("rF", "lF", "aF")
    wait(qc, aY, oY)
    fire(C.dma_start(T.syms[:, 0:512], T.lY[:]), "out2", 16)
    wait(qc, aZ, oZ)
    fire(C.dma_start(T.syms[:, 512:768], T.lZ[:]), "out2", 16)
    wait(qy, aF, oFl)
    fire(Y.dma_start(T.last[:], T.lF[:, 64:128, :]), "out1", 16)
    wait(qc, aF, oF3)
    fire(C.dma_start(T.syms[:, 768:1024], T.lF[:, 0:64, :]), "out2", 16)
    for name in count:
        if seen.get(name, 0) < count[name]:
            wait(qg, (name, count[name]))
